import numpy as np
import ml_dtypes


def mxq(x, axis, fmt="e4m3"):
    dtype, down = {"e4m3": (ml_dtypes.float8_e4m3fn, 7), "e5m2": (ml_dtypes.float8_e5m2, 14)}[fmt]
    v = np.moveaxis(np.asarray(x, np.float32).astype(ml_dtypes.bfloat16).astype(np.float64), axis, -1)
    blocks = v.reshape(v.shape[:-1] + (-1, 32))
    amax = np.abs(blocks).max(-1, keepdims=True)
    byte = np.maximum(np.where(amax > 0, np.frexp(amax)[1] - 1 + 127, 0) - down, 1)
    scale = np.exp2(byte - 127.0)
    codes = (blocks / scale).astype(np.float32).astype(dtype).astype(np.float64)
    return np.moveaxis((codes * scale).reshape(v.shape), -1, axis)


WIDE = False


def mx_kscale(k):
    if not WIDE:
        return np.ones(k)
    levels = np.array([10, -10, 5, -5, 0])
    if k % 512:
        return np.exp2(np.random.permutation(np.resize(levels, k // 32))).repeat(32)
    a = np.empty((k // 512, 16))
    for p in range(k // 512):
        a[p, :8] = np.random.permutation(np.resize(levels, 8))
        for g in range(8):
            far = levels[np.abs(levels - a[p, g]) >= 10]
            a[p, g + 8] = far[np.random.randint(len(far))]
    return np.exp2(a.ravel()).repeat(32)


def f64(x):
    return np.asarray(x).astype(np.float64)


def striped(idx):
    return np.tile(idx.reshape(-1, 16).T, (8, 1)).astype(np.uint16)


def unstriped(offs):
    return offs[:16].T.reshape(-1).astype(np.int64)


def pack_weight(w):
    k, n = w.shape
    w = f64(np.asarray(w, np.float32).astype(ml_dtypes.bfloat16)).reshape(k // 32, 32, n)
    amax = np.abs(w).max(1)
    byte = np.clip(np.where(amax > 0, np.frexp(amax)[1] - 1 + 127 - 7, 1), 1, 254)
    scaled = (w * np.exp2(127.0 - byte)[:, None, :]).reshape(k, n).astype(np.float32)
    words = np.ascontiguousarray(scaled.reshape(k // 512, 128, 4, n).transpose(0, 1, 3, 2)).astype(ml_dtypes.float8_e4m3fn).view(np.uint8)
    return words, np.ascontiguousarray(byte.astype(np.uint8).reshape(k // 512, 16, n))


def unpack_weight(words, scales):
    g, p, n, _ = words.shape
    vals = np.ascontiguousarray(words).view(ml_dtypes.float8_e4m3fn).astype(np.float64) * np.repeat(np.exp2(scales.astype(np.float64) - 127.0), 8, axis=1)[..., None]
    return vals.transpose(0, 1, 3, 2).reshape(g * 512, n)


def relu(v):
    return np.maximum(v, 0.0)


K, T, S, D, V, H, N = 512, 1024, 512, 2, 256, 512, 128
P = 2 ** 7


def setup_inputs():
    n = np.random.standard_normal
    s = mx_kscale(K)[:, None]
    u = mx_kscale(H)
    near = np.random.permutation(S)
    packed_xT = pack_weight(n((K, T)) * s)
    packed_w2 = pack_weight(n((H, N)) / np.sqrt(2 * H) / u[:, None])
    packed_w3 = pack_weight(n((K, N)) / np.sqrt(2 * K) / s)
    return {
        "x_words": packed_xT[0],
        "x_scales": packed_xT[1],
        "w1": (n((K, H)) / np.sqrt(K) / s * u).astype(np.float32),
        "w2_words": packed_w2[0],
        "w2_scales": packed_w2[1],
        "gate": (np.tile(np.random.uniform(0.2, 1.0, (D, 1, V)) / np.sqrt(D), (1, P, 1))).astype(np.float32),
        "eT": (n((K, V)) * s).astype(np.float32),
        "w3_words": packed_w3[0],
        "w3_scales": packed_w3[1],
        "offs": striped(np.random.permutation(T)[:S]),
        "pos1": striped(near[:V]),
        "pos2": striped(near[V:]),
    }


def reference(x_words, x_scales, w1, w2_words, w2_scales, gate, eT, w3_words, w3_scales, offs, pos1, pos2):
    xq = unpack_weight(x_words, x_scales)[:, unstriped(offs)]
    h = relu(mxq(f64(w1), 0, "e4m3").T @ xq)
    z = h[:, unstriped(pos1)] * f64(gate)[0, :1] + h[:, unstriped(pos2)] * f64(gate)[1, :1]
    eTq = mxq(f64(eT), 0, "e4m3")
    return unpack_weight(w2_words, w2_scales).T @ mxq(z, 0, "e4m3") + unpack_weight(w3_words, w3_scales).T @ eTq

@@ -1,0 +1,185 @@
+from contextlib import ExitStack
+
+import concourse.mybir as mybir
+
+K, T, S, V, H, N = 512, 1024, 512, 256, 512, 128
+P = 128
+PACK = 4
+FLOPS = 2 * K * H * S + 2 * H * N * V + 2 * K * N * V
+
+F32 = mybir.dt.float32
+BF16 = mybir.dt.bfloat16
+I32 = mybir.dt.int32
+U32 = mybir.dt.uint32
+U16 = mybir.dt.uint16
+U8 = mybir.dt.uint8
+FP8X4 = mybir.dt.float8_e4m3fn_x4
+ALU = mybir.AluOpType
+RELU = mybir.ActivationFunctionType.Relu
+
+W_CHUNKS = 2
+W_COLS = H // W_CHUNKS
+W_VECTOR = 44
+
+
+def tile_picked_zfp_lin_p_kernel(
+    tc, x_words, x_scales, w1, w2_words, w2_scales, gate, eT, w3_words, w3_scales, offs, pos1, pos2, out
+):
+    nc = tc.nc
+    with ExitStack() as ctx:
+        keep = ctx.enter_context(tc.tile_pool(name="keep", bufs=1))
+        psum = ctx.enter_context(tc.psum_pool(name="psum", bufs=1))
+
+        def sbuf(name, shape, dtype):
+            return keep.tile(shape, dtype, name=name, align_bytes=64)
+
+        def words_of(packed):
+            return packed[0].rearrange("p c r -> p (c r)").bitcast(I32)
+
+        def load_scales(queue, plane, scales):
+            for q in range(4):
+                queue.dma_start(plane[32 * q : 32 * q + 4, :].bitcast(I32), scales[0, 4 * q : 4 * q + 4, :].bitcast(I32))
+
+        offs_sb = sbuf("offs_sb", [P, S // 16], U16)
+        pos_sb = [sbuf(f"pos_sb{d}", [P, V // 16], U16) for d in range(2)]
+        xw_all = sbuf("xw_all", [P, T], I32)
+        xs_all = sbuf("xs_all", [P, T], U8)
+        w1_raw = [sbuf(f"w1_raw{c}", [P, PACK, W_COLS], F32) for c in range(W_CHUNKS)]
+        gate_sb = sbuf("gate_sb", [P, 2, V], F32)
+        e_raw = sbuf("e_raw", [P, PACK, V], F32)
+        w2w = sbuf("w2w", [P, N], I32)
+        w3w = sbuf("w3w", [P, N], I32)
+        w2s = sbuf("w2s", [P, N], U8)
+        w3s = sbuf("w3s", [P, N], U8)
+
+        nc.gpsimd.memset(xs_all[:].bitcast(I32), 0)
+        nc.gpsimd.memset(w3s[:].bitcast(I32), 0)
+        nc.gpsimd.memset(w2s[:].bitcast(I32), 0)
+
+        nc.sync.dma_start(offs_sb[:], offs)
+        w1_rows = w1.rearrange("(p j) c -> p j c", j=PACK)
+        for c in range(W_CHUNKS):
+            nc.sync.dma_start(w1_raw[c][:], w1_rows[:, :, c * W_COLS : (c + 1) * W_COLS])
+            if c == 0:
+                load_scales(nc.sync, xs_all, x_scales)
+        nc.sync.dma_start(xw_all[:], words_of(x_words))
+        nc.sync.dma_start(pos_sb[0][:], pos1)
+        nc.sync.dma_start(pos_sb[1][:], pos2)
+        nc.sync.dma_start(gate_sb[:], gate.rearrange("d p v -> p d v"))
+        nc.sync.dma_start(e_raw[:], eT.rearrange("(p j) v -> p j v", j=PACK))
+        nc.sync.dma_start(w3w[:], words_of(w3_words))
+        nc.sync.dma_start(w2w[:], words_of(w2_words))
+        load_scales(nc.sync, w3s, w3_scales)
+        load_scales(nc.sync, w2s, w2_scales)
+
+        xs = sbuf("xs", [P, S], U8)
+        nc.vector.tensor_copy(xs[:], xs_all[:].indirect(offs_sb[:]))
+
+        w1_bf = sbuf("w1_bf", [P, PACK, P, PACK], BF16)
+        m_per = W_COLS // PACK
+        for c in range(W_CHUNKS):
+            dst = w1_bf[:].rearrange("p t m j -> p m t j")[:, c * m_per : (c + 1) * m_per]
+            src = w1_raw[c][:].rearrange("p j (m t) -> p m t j", t=PACK)
+            if c < W_CHUNKS - 1:
+                nc.scalar.copy(dst, src)
+            else:
+                nc.vector.tensor_copy(dst[:, :W_VECTOR], src[:, :W_VECTOR])
+                nc.scalar.copy(dst[:, W_VECTOR:], src[:, W_VECTOR:])
+
+        w1_codes = [sbuf(f"w1_codes{t}", [P, P], U32) for t in range(PACK)]
+        w1_scale = [sbuf(f"w1_scale{t}", [P, P], U8) for t in range(PACK)]
+
+        def quantize_w1(t):
+            nc.vector.quantize_mx(
+                w1_codes[t][:].bitcast(FP8X4), w1_scale[t][:], w1_bf[:, t].rearrange("p m j -> p (m j)")
+            )
+
+        half = S // 2
+        xw = sbuf("xw", [P, S], U32)
+        quantize_w1(0)
+        for u in range(2):
+            nc.vector.tensor_copy(
+                xw[:, u * half : (u + 1) * half],
+                xw_all[:].bitcast(U32).indirect(offs_sb[:, u * half // 16 : (u + 1) * half // 16]),
+            )
+        for t in range(1, PACK):
+            quantize_w1(t)
+
+        def first_product(t, bank, cols):
+            nc.tensor.matmul_mx(
+                bank,
+                lhsT=w1_codes[t][:].bitcast(FP8X4),
+                lhsT_scale=w1_scale[t][:],
+                rhs=xw[:, cols].bitcast(FP8X4),
+                rhs_scale=xs[:, cols],
+                start=True,
+                stop=True,
+            )
+
+        h = [sbuf(f"h{t}", [P, S], F32) for t in range(PACK)]
+        h0_banks = [psum.tile([P, half], F32, name=f"h0_bank{u}") for u in range(2)]
+        for u in range(2):
+            first_product(0, h0_banks[u][:], slice(u * half, (u + 1) * half))
+        nc.scalar.activation(h[0][:, :half], h0_banks[0][:], RELU)
+        nc.vector.tensor_scalar(h[0][:, half:], h0_banks[1][:], 0.0, None, ALU.max)
+        for t in range(1, PACK):
+            bank = psum.tile([P, S], F32, name=f"h_bank{t}")
+            first_product(t, bank[:], slice(0, S))
+            nc.scalar.activation(h[t][:], bank[:], RELU)
+
+        e_bf = sbuf("e_bf", [P, V, PACK], BF16)
+        nc.scalar.copy(
+            e_bf[:].rearrange("p (c i) j -> p c j i", i=4), e_raw[:].rearrange("p j (c i) -> p c j i", i=4)
+        )
+
+        terms = [sbuf(f"terms{d}", [P, PACK, V], F32) for d in range(2)]
+        for t in range(PACK):
+            for d in range(2):
+                nc.vector.tensor_tensor(terms[d][:, t, :], h[t][:].indirect(pos_sb[d][:]), gate_sb[:, d, :], ALU.mult)
+
+        e_codes = sbuf("e_codes", [P, V], U32)
+        e_scale = sbuf("e_scale", [P, V], U8)
+        nc.vector.quantize_mx(e_codes[:].bitcast(FP8X4), e_scale[:], e_bf[:].rearrange("p v j -> p (v j)"))
+
+        vh = V // 2
+        z_bf = [sbuf(f"z_bf{u}", [P, vh, PACK], BF16) for u in range(2)]
+        z_codes = [sbuf(f"z_codes{u}", [P, vh], U32) for u in range(2)]
+        z_scale = [sbuf(f"z_scale{u}", [P, vh], U8) for u in range(2)]
+        for u in range(2):
+            cols = slice(u * vh, (u + 1) * vh)
+            nc.vector.tensor_tensor(
+                z_bf[u][:].rearrange("p (c i) t -> p c t i", i=4),
+                terms[0][:, :, cols].rearrange("p t (c i) -> p c t i", i=4),
+                terms[1][:, :, cols].rearrange("p t (c i) -> p c t i", i=4),
+                ALU.add,
+            )
+        for u in range(2):
+            nc.vector.quantize_mx(z_codes[u][:].bitcast(FP8X4), z_scale[u][:], z_bf[u][:].rearrange("p v t -> p (v t)"))
+        for u in range(2):
+            cols = slice(u * vh, (u + 1) * vh)
+            bank = psum.tile([P, vh], F32, name=f"out_bank{u}")
+            nc.tensor.matmul_mx(
+                bank[:],
+                lhsT=w3w[:].bitcast(FP8X4),
+                lhsT_scale=w3s[:],
+                rhs=e_codes[:, cols].bitcast(FP8X4),
+                rhs_scale=e_scale[:, cols],
+                start=True,
+                stop=False,
+            )
+            nc.tensor.matmul_mx(
+                bank[:],
+                lhsT=w2w[:].bitcast(FP8X4),
+                lhsT_scale=w2s[:],
+                rhs=z_codes[u][:].bitcast(FP8X4),
+                rhs_scale=z_scale[u][:],
+                start=False,
+                stop=True,
+            )
+            result = sbuf(f"result{u}", [P, vh], F32)
+            if u == 0:
+                nc.scalar.copy(result[:], bank[:])
+                nc.scalar.dma_start(out[:, cols], result[:])
+            else:
+                nc.vector.tensor_copy(result[:], bank[:])
+                nc.sync.dma_start(out[:, cols], result[:])

@@ -1,6 +1,7 @@
 from contextlib import ExitStack
 
 import concourse.mybir as mybir
+from concourse.masks import make_identity
 
 K, T, S, V, H, N = 512, 1024, 512, 256, 512, 128
 P = 128
@@ -16,10 +17,12 @@ U8 = mybir.dt.uint8
 FP8X4 = mybir.dt.float8_e4m3fn_x4
 ALU = mybir.AluOpType
 RELU = mybir.ActivationFunctionType.Relu
+COPY = mybir.ActivationFunctionType.Copy
+VH = V // 2
 
-W_CHUNKS = 2
+W_CHUNKS = 4
 W_COLS = H // W_CHUNKS
-W_VECTOR = 44
+W_VECTOR = 20
 
 
 def tile_picked_zfp_lin_p_kernel(
@@ -30,8 +33,8 @@ def tile_picked_zfp_lin_p_kernel(
         keep = ctx.enter_context(tc.tile_pool(name="keep", bufs=1))
         psum = ctx.enter_context(tc.psum_pool(name="psum", bufs=1))
 
-        def sbuf(name, shape, dtype):
-            return keep.tile(shape, dtype, name=name, align_bytes=64)
+        def sbuf(name, shape, dtype, tag=""):
+            return keep.tile(shape, dtype, name=name, align_bytes=64, tag=tag)
 
         def words_of(packed):
             return packed[0].rearrange("p c r -> p (c r)").bitcast(I32)
@@ -45,7 +48,9 @@ def tile_picked_zfp_lin_p_kernel(
         xw_all = sbuf("xw_all", [P, T], I32)
         xs_all = sbuf("xs_all", [P, T], U8)
         w1_raw = [sbuf(f"w1_raw{c}", [P, PACK, W_COLS], F32) for c in range(W_CHUNKS)]
-        gate_sb = sbuf("gate_sb", [P, 2, V], F32)
+        gate_rows = sbuf("gate_rows", [P, 2, VH], F32)
+        gate_cols = sbuf("gate_cols", [P, 2], F32)
+        identity = sbuf("identity", [P, P], F32)
         e_raw = sbuf("e_raw", [P, PACK, V], F32)
         w2w = sbuf("w2w", [P, N], I32)
         w3w = sbuf("w3w", [P, N], I32)
@@ -55,6 +60,7 @@ def tile_picked_zfp_lin_p_kernel(
         nc.gpsimd.memset(xs_all[:].bitcast(I32), 0)
         nc.gpsimd.memset(w3s[:].bitcast(I32), 0)
         nc.gpsimd.memset(w2s[:].bitcast(I32), 0)
+        make_identity(nc, identity[:])
 
         nc.sync.dma_start(offs_sb[:], offs)
         w1_rows = w1.rearrange("(p j) c -> p j c", j=PACK)
@@ -62,11 +68,13 @@ def tile_picked_zfp_lin_p_kernel(
             nc.sync.dma_start(w1_raw[c][:], w1_rows[:, :, c * W_COLS : (c + 1) * W_COLS])
             if c == 0:
                 load_scales(nc.sync, xs_all, x_scales)
-        nc.sync.dma_start(xw_all[:], words_of(x_words))
+                nc.sync.dma_start(xw_all[:], words_of(x_words))
         nc.sync.dma_start(pos_sb[0][:], pos1)
         nc.sync.dma_start(pos_sb[1][:], pos2)
-        nc.sync.dma_start(gate_sb[:], gate.rearrange("d p v -> p d v"))
         nc.sync.dma_start(e_raw[:], eT.rearrange("(p j) v -> p j v", j=PACK))
+        with nc.allow_non_contiguous_dma(reason="one gate value a partition"):
+            nc.sync.dma_start(gate_cols[:], gate[:, 0, :VH].rearrange("d v -> v d"))
+        nc.sync.dma_start(gate_rows[:], gate[:, :, VH:].rearrange("d p v -> p d v"))
         nc.sync.dma_start(w3w[:], words_of(w3_words))
         nc.sync.dma_start(w2w[:], words_of(w2_words))
         load_scales(nc.sync, w3s, w3_scales)
@@ -75,13 +83,18 @@ def tile_picked_zfp_lin_p_kernel(
         xs = sbuf("xs", [P, S], U8)
         nc.vector.tensor_copy(xs[:], xs_all[:].indirect(offs_sb[:]))
 
+        xw = sbuf("xw", [P, S], U32)
+        nc.vector.tensor_copy(xw[:], xw_all[:].bitcast(U32).indirect(offs_sb[:]))
+
         w1_bf = sbuf("w1_bf", [P, PACK, P, PACK], BF16)
         m_per = W_COLS // PACK
         for c in range(W_CHUNKS):
             dst = w1_bf[:].rearrange("p t m j -> p m t j")[:, c * m_per : (c + 1) * m_per]
             src = w1_raw[c][:].rearrange("p j (m t) -> p m t j", t=PACK)
-            if c < W_CHUNKS - 1:
+            if c < 2:
                 nc.scalar.copy(dst, src)
+            elif c == 2:
+                nc.vector.tensor_copy(dst, src)
             else:
                 nc.vector.tensor_copy(dst[:, :W_VECTOR], src[:, :W_VECTOR])
                 nc.scalar.copy(dst[:, W_VECTOR:], src[:, W_VECTOR:])
@@ -95,14 +108,7 @@ def tile_picked_zfp_lin_p_kernel(
             )
 
         half = S // 2
-        xw = sbuf("xw", [P, S], U32)
-        quantize_w1(0)
-        for u in range(2):
-            nc.vector.tensor_copy(
-                xw[:, u * half : (u + 1) * half],
-                xw_all[:].bitcast(U32).indirect(offs_sb[:, u * half // 16 : (u + 1) * half // 16]),
-            )
-        for t in range(1, PACK):
+        for t in range(PACK):
             quantize_w1(t)
 
         def first_product(t, bank, cols):
@@ -117,7 +123,7 @@ def tile_picked_zfp_lin_p_kernel(
             )
 
         h = [sbuf(f"h{t}", [P, S], F32) for t in range(PACK)]
-        h0_banks = [psum.tile([P, half], F32, name=f"h0_bank{u}") for u in range(2)]
+        h0_banks = [psum.tile([P, half], F32, name=f"h0_bank{u}", tag=f"half_bank{u}") for u in range(2)]
         for u in range(2):
             first_product(0, h0_banks[u][:], slice(u * half, (u + 1) * half))
         nc.scalar.activation(h[0][:, :half], h0_banks[0][:], RELU)
@@ -127,37 +133,22 @@ def tile_picked_zfp_lin_p_kernel(
             first_product(t, bank[:], slice(0, S))
             nc.scalar.activation(h[t][:], bank[:], RELU)
 
-        e_bf = sbuf("e_bf", [P, V, PACK], BF16)
-        nc.scalar.copy(
-            e_bf[:].rearrange("p (c i) j -> p c j i", i=4), e_raw[:].rearrange("p j (c i) -> p c j i", i=4)
-        )
-
-        terms = [sbuf(f"terms{d}", [P, PACK, V], F32) for d in range(2)]
-        for t in range(PACK):
-            for d in range(2):
-                nc.vector.tensor_tensor(terms[d][:, t, :], h[t][:].indirect(pos_sb[d][:]), gate_sb[:, d, :], ALU.mult)
-
+        e_bf = sbuf("e_bf", [P, V, PACK], BF16, tag="late1")
+        for u in range(2):
+            cols = slice(u * VH, (u + 1) * VH)
+            nc.scalar.copy(
+                e_bf[:, cols].rearrange("p (c i) j -> p c j i", i=4),
+                e_raw[:, :, cols].rearrange("p j (c i) -> p c j i", i=4),
+            )
         e_codes = sbuf("e_codes", [P, V], U32)
         e_scale = sbuf("e_scale", [P, V], U8)
-        nc.vector.quantize_mx(e_codes[:].bitcast(FP8X4), e_scale[:], e_bf[:].rearrange("p v j -> p (v j)"))
 
-        vh = V // 2
-        z_bf = [sbuf(f"z_bf{u}", [P, vh, PACK], BF16) for u in range(2)]
-        z_codes = [sbuf(f"z_codes{u}", [P, vh], U32) for u in range(2)]
-        z_scale = [sbuf(f"z_scale{u}", [P, vh], U8) for u in range(2)]
-        for u in range(2):
-            cols = slice(u * vh, (u + 1) * vh)
-            nc.vector.tensor_tensor(
-                z_bf[u][:].rearrange("p (c i) t -> p c t i", i=4),
-                terms[0][:, :, cols].rearrange("p t (c i) -> p c t i", i=4),
-                terms[1][:, :, cols].rearrange("p t (c i) -> p c t i", i=4),
-                ALU.add,
-            )
-        for u in range(2):
-            nc.vector.quantize_mx(z_codes[u][:].bitcast(FP8X4), z_scale[u][:], z_bf[u][:].rearrange("p v t -> p (v t)"))
-        for u in range(2):
-            cols = slice(u * vh, (u + 1) * vh)
-            bank = psum.tile([P, vh], F32, name=f"out_bank{u}")
+        def second_product(u, z_bf):
+            cols = slice(u * VH, (u + 1) * VH)
+            z_codes = sbuf(f"z_codes{u}", [P, VH], U32)
+            z_scale = sbuf(f"z_scale{u}", [P, VH], U8)
+            nc.vector.quantize_mx(z_codes[:].bitcast(FP8X4), z_scale[:], z_bf[:].rearrange("p v t -> p (v t)"))
+            bank = psum.tile([P, VH], F32, name=f"out_bank{u}", tag=f"half_bank{u}")
             nc.tensor.matmul_mx(
                 bank[:],
                 lhsT=w3w[:].bitcast(FP8X4),
@@ -171,15 +162,60 @@ def tile_picked_zfp_lin_p_kernel(
                 bank[:],
                 lhsT=w2w[:].bitcast(FP8X4),
                 lhsT_scale=w2s[:],
-                rhs=z_codes[u][:].bitcast(FP8X4),
-                rhs_scale=z_scale[u][:],
+                rhs=z_codes[:].bitcast(FP8X4),
+                rhs_scale=z_scale[:],
                 start=False,
                 stop=True,
             )
-            result = sbuf(f"result{u}", [P, vh], F32)
+            result = sbuf(f"result{u}", [P, VH], F32)
             if u == 0:
                 nc.scalar.copy(result[:], bank[:])
-                nc.scalar.dma_start(out[:, cols], result[:])
             else:
                 nc.vector.tensor_copy(result[:], bank[:])
-                nc.sync.dma_start(out[:, cols], result[:])
+            nc.sync.dma_start(out[:, cols], result[:])
+
+        lists = VH // 16
+        picked = [
+            [sbuf(f"picked{t}_{d}", [P, VH], F32, tag="late0" if (t, d) == (2, 1) else "") for d in range(2)] for t in range(PACK)
+        ]
+        for t in range(PACK):
+            for d in range(2):
+                nc.vector.tensor_copy(picked[t][d][:], h[t][:].indirect(pos_sb[d][:, :lists]))
+        z_bank = psum.tile([P, PACK, VH], F32, name="z_bank")
+        for pair in range(2):
+            turned = psum.tile([P, 2, 2, P], F32, name=f"turned{pair}")
+            gated = sbuf(f"gated{pair}", [P, 2, 2, P], F32)
+            for k in range(2):
+                for d in range(2):
+                    nc.tensor.transpose(turned[:, d, k, :], picked[2 * pair + k][d][:], identity[:])
+            for d in range(2):
+                nc.scalar.activation(gated[:, d], turned[:, d], COPY, scale=gate_cols[:, d : d + 1])
+            for k in range(2):
+                for d in range(2):
+                    nc.tensor.matmul(
+                        z_bank[:, 2 * pair + k, :],
+                        lhsT=gated[:, d, k, :],
+                        rhs=identity[:],
+                        is_transpose=True,
+                        start=(d == 0),
+                        stop=(d == 1),
+                    )
+        z_first = sbuf("z_first", [P, VH, PACK], BF16, tag="z_bf")
+        nc.scalar.copy(z_first[:], z_bank[:].rearrange("p t v -> p v t"))
+
+        nc.vector.quantize_mx(e_codes[:].bitcast(FP8X4), e_scale[:], e_bf[:].rearrange("p v j -> p (v j)"))
+        terms = [sbuf(f"terms{d}", [P, PACK, VH], F32, tag=f"late{d}") for d in range(2)]
+        for t in range(PACK):
+            for d in range(2):
+                nc.vector.tensor_tensor(
+                    terms[d][:, t, :], h[t][:].indirect(pos_sb[d][:, lists:]), gate_rows[:, d, :], ALU.mult
+                )
+        second_product(0, z_first)
+        z_second = sbuf("z_second", [P, VH, PACK], BF16, tag="z_bf")
+        nc.vector.tensor_tensor(
+            z_second[:].rearrange("p (c i) t -> p c t i", i=4),
+            terms[0][:].rearrange("p t (c i) -> p c t i", i=4),
+            terms[1][:].rearrange("p t (c i) -> p c t i", i=4),
+            ALU.add,
+        )
+        second_product(1, z_second)

@@ -22,7 +22,7 @@ VH = V // 2
 
 W_CHUNKS = 4
 W_COLS = H // W_CHUNKS
-W_VECTOR = 20
+W_VECTOR = 16
 
 
 def tile_picked_zfp_lin_p_kernel(
@@ -63,12 +63,11 @@ def tile_picked_zfp_lin_p_kernel(
         make_identity(nc, identity[:])
 
         nc.sync.dma_start(offs_sb[:], offs)
+        nc.sync.dma_start(xw_all[:], words_of(x_words))
+        load_scales(nc.sync, xs_all, x_scales)
         w1_rows = w1.rearrange("(p j) c -> p j c", j=PACK)
         for c in range(W_CHUNKS):
             nc.sync.dma_start(w1_raw[c][:], w1_rows[:, :, c * W_COLS : (c + 1) * W_COLS])
-            if c == 0:
-                load_scales(nc.sync, xs_all, x_scales)
-                nc.sync.dma_start(xw_all[:], words_of(x_words))
         nc.sync.dma_start(pos_sb[0][:], pos1)
         nc.sync.dma_start(pos_sb[1][:], pos2)
         nc.sync.dma_start(e_raw[:], eT.rearrange("(p j) v -> p j v", j=PACK))
@@ -80,11 +79,10 @@ def tile_picked_zfp_lin_p_kernel(
         load_scales(nc.sync, w3s, w3_scales)
         load_scales(nc.sync, w2s, w2_scales)
 
-        xs = sbuf("xs", [P, S], U8)
-        nc.vector.tensor_copy(xs[:], xs_all[:].indirect(offs_sb[:]))
-
         xw = sbuf("xw", [P, S], U32)
         nc.vector.tensor_copy(xw[:], xw_all[:].bitcast(U32).indirect(offs_sb[:]))
+        xs = sbuf("xs", [P, S], U8)
+        nc.vector.tensor_copy(xs[:], xs_all[:].indirect(offs_sb[:]))
 
         w1_bf = sbuf("w1_bf", [P, PACK, P, PACK], BF16)
         m_per = W_COLS // PACK
@@ -93,7 +91,7 @@ def tile_picked_zfp_lin_p_kernel(
             src = w1_raw[c][:].rearrange("p j (m t) -> p m t j", t=PACK)
             if c < 2:
                 nc.scalar.copy(dst, src)
-            elif c == 2:
+            elif c == 3:
                 nc.vector.tensor_copy(dst, src)
             else:
                 nc.vector.tensor_copy(dst[:, :W_VECTOR], src[:, :W_VECTOR])

@@ -20,9 +20,9 @@ RELU = mybir.ActivationFunctionType.Relu
 COPY = mybir.ActivationFunctionType.Copy
 VH = V // 2
 
-W_CHUNKS = 4
+W_CHUNKS = 2
 W_COLS = H // W_CHUNKS
-W_VECTOR = 16
+W_VECTOR = 52
 
 
 def tile_picked_zfp_lin_p_kernel(
@@ -89,15 +89,13 @@ def tile_picked_zfp_lin_p_kernel(
         for c in range(W_CHUNKS):
             dst = w1_bf[:].rearrange("p t m j -> p m t j")[:, c * m_per : (c + 1) * m_per]
             src = w1_raw[c][:].rearrange("p j (m t) -> p m t j", t=PACK)
-            if c < 2:
+            if c == 0:
                 nc.scalar.copy(dst, src)
-            elif c == 3:
-                nc.vector.tensor_copy(dst, src)
             else:
                 nc.vector.tensor_copy(dst[:, :W_VECTOR], src[:, :W_VECTOR])
                 nc.scalar.copy(dst[:, W_VECTOR:], src[:, W_VECTOR:])
 
-        w1_codes = [sbuf(f"w1_codes{t}", [P, P], U32) for t in range(PACK)]
+        w1_codes = [sbuf(f"w1_codes{t}", [P, P], U32, tag="late1" if t == PACK - 1 else "") for t in range(PACK)]
         w1_scale = [sbuf(f"w1_scale{t}", [P, P], U8) for t in range(PACK)]
 
         def quantize_w1(t):

@@ -22,7 +22,6 @@ VH = V // 2
 
 W_CHUNKS = 2
 W_COLS = H // W_CHUNKS
-W_VECTOR = 52
 
 
 def tile_picked_zfp_lin_p_kernel(
@@ -48,8 +47,8 @@ def tile_picked_zfp_lin_p_kernel(
         xw_all = sbuf("xw_all", [P, T], I32)
         xs_all = sbuf("xs_all", [P, T], U8)
         w1_raw = [sbuf(f"w1_raw{c}", [P, PACK, W_COLS], F32) for c in range(W_CHUNKS)]
-        gate_rows = sbuf("gate_rows", [P, 2, VH], F32)
-        gate_cols = sbuf("gate_cols", [P, 2], F32)
+        gate_rows = [sbuf(f"gate_rows{d}", [P, V], F32, tag=f"gate_slot{d}") for d in range(2)]
+        gate_cols = [sbuf(f"gate_cols{d}", [P, 2], F32) for d in range(2)]
         identity = sbuf("identity", [P, P], F32)
         e_raw = sbuf("e_raw", [P, PACK, V], F32)
         w2w = sbuf("w2w", [P, N], I32)
@@ -72,8 +71,10 @@ def tile_picked_zfp_lin_p_kernel(
         nc.sync.dma_start(pos_sb[1][:], pos2)
         nc.sync.dma_start(e_raw[:], eT.rearrange("(p j) v -> p j v", j=PACK))
         with nc.allow_non_contiguous_dma(reason="one gate value a partition"):
-            nc.sync.dma_start(gate_cols[:], gate[:, 0, :VH].rearrange("d v -> v d"))
-        nc.sync.dma_start(gate_rows[:], gate[:, :, VH:].rearrange("d p v -> p d v"))
+            for d in range(2):
+                nc.sync.dma_start(gate_cols[d][:], gate[d, 0, :].rearrange("(u v) -> v u", u=2))
+        for d in range(2):
+            nc.sync.dma_start(gate_rows[d][:], gate[d])
         nc.sync.dma_start(w3w[:], words_of(w3_words))
         nc.sync.dma_start(w2w[:], words_of(w2_words))
         load_scales(nc.sync, w3s, w3_scales)
@@ -92,8 +93,8 @@ def tile_picked_zfp_lin_p_kernel(
             if c == 0:
                 nc.scalar.copy(dst, src)
             else:
-                nc.vector.tensor_copy(dst[:, :W_VECTOR], src[:, :W_VECTOR])
-                nc.scalar.copy(dst[:, W_VECTOR:], src[:, W_VECTOR:])
+                nc.vector.tensor_copy(dst[:, :, :2], src[:, :, :2])
+                nc.scalar.copy(dst[:, :, 2:], src[:, :, 2:])
 
         w1_codes = [sbuf(f"w1_codes{t}", [P, P], U32, tag="late1" if t == PACK - 1 else "") for t in range(PACK)]
         w1_scale = [sbuf(f"w1_scale{t}", [P, P], U8) for t in range(PACK)]
@@ -122,28 +123,74 @@ def tile_picked_zfp_lin_p_kernel(
         h0_banks = [psum.tile([P, half], F32, name=f"h0_bank{u}", tag=f"half_bank{u}") for u in range(2)]
         for u in range(2):
             first_product(0, h0_banks[u][:], slice(u * half, (u + 1) * half))
-        nc.scalar.activation(h[0][:, :half], h0_banks[0][:], RELU)
-        nc.vector.tensor_scalar(h[0][:, half:], h0_banks[1][:], 0.0, None, ALU.max)
+        nc.vector.tensor_scalar(h[0][:, :half], h0_banks[0][:], 0.0, None, ALU.max)
+        nc.scalar.activation(h[0][:, half:], h0_banks[1][:], RELU)
         for t in range(1, PACK):
-            bank = psum.tile([P, S], F32, name=f"h_bank{t}")
+            bank = psum.tile([P, S], F32, name=f"h_bank{t}", tag=f"h_slot{t}")
             first_product(t, bank[:], slice(0, S))
             nc.scalar.activation(h[t][:], bank[:], RELU)
 
         e_bf = sbuf("e_bf", [P, V, PACK], BF16, tag="late1")
-        for u in range(2):
+
+        def round_e(u):
             cols = slice(u * VH, (u + 1) * VH)
             nc.scalar.copy(
                 e_bf[:, cols].rearrange("p (c i) j -> p c j i", i=4),
                 e_raw[:, :, cols].rearrange("p j (c i) -> p c j i", i=4),
             )
-        e_codes = sbuf("e_codes", [P, V], U32)
-        e_scale = sbuf("e_scale", [P, V], U8)
 
-        def second_product(u, z_bf):
+        round_e(0)
+        z_bf = [sbuf(f"z_bf{u}", [P, VH, PACK], BF16) for u in range(2)]
+
+        picked = [[sbuf(f"picked{t}_{d}", [P, V], F32) for d in range(2)] for t in range(2)]
+        for t in range(2):
+            for d in range(2):
+                nc.vector.tensor_copy(picked[t][d][:], h[t][:].indirect(pos_sb[d][:]))
+        gated = []
+        for d in range(2):
+            turned = psum.tile([P, 2, 2, P], F32, name=f"turned{d}")
+            gated.append(sbuf(f"gated{d}", [P, 2, 2, P], F32))
+            for t in range(2):
+                for u in range(2):
+                    nc.tensor.transpose(turned[:, u, t, :], picked[t][d][:, u * VH : (u + 1) * VH], identity[:])
+            for u in range(2):
+                nc.scalar.activation(gated[d][:, u], turned[:, u], COPY, scale=gate_cols[d][:, u : u + 1])
+        round_e(1)
+        for u in range(2):
+            z_bank = psum.tile([P, 2, VH], F32, name=f"z_bank{u}", tag=f"h_slot{u + 1}")
+            for t in range(2):
+                for d in range(2):
+                    nc.tensor.matmul(
+                        z_bank[:, t, :],
+                        lhsT=gated[d][:, u, t, :],
+                        rhs=identity[:],
+                        is_transpose=True,
+                        start=(d == 0),
+                        stop=(d == 1),
+                    )
+            nc.scalar.copy(z_bf[u][:, :, 0:2], z_bank[:].rearrange("p t v -> p v t"))
+
+        terms = [sbuf(f"terms{d}", [P, 2, V], F32) for d in range(2)]
+        for t in range(2):
+            for d in range(2):
+                nc.vector.tensor_tensor(terms[d][:, t, :], h[2 + t][:].indirect(pos_sb[d][:]), gate_rows[d][:], ALU.mult)
+
+        e_codes = sbuf("e_codes", [P, V], U32, tag="gate_slot0")
+        e_scale = sbuf("e_scale", [P, V], U8)
+        nc.vector.quantize_mx(e_codes[:].bitcast(FP8X4), e_scale[:], e_bf[:].rearrange("p v j -> p (v j)"))
+        for u in range(2):
+            cols = slice(u * VH, (u + 1) * VH)
+            nc.vector.tensor_tensor(
+                z_bf[u][:, :, 2:4],
+                terms[0][:, :, cols].rearrange("p t v -> p v t"),
+                terms[1][:, :, cols].rearrange("p t v -> p v t"),
+                ALU.add,
+            )
+        for u in range(2):
             cols = slice(u * VH, (u + 1) * VH)
             z_codes = sbuf(f"z_codes{u}", [P, VH], U32)
             z_scale = sbuf(f"z_scale{u}", [P, VH], U8)
-            nc.vector.quantize_mx(z_codes[:].bitcast(FP8X4), z_scale[:], z_bf[:].rearrange("p v t -> p (v t)"))
+            nc.vector.quantize_mx(z_codes[:].bitcast(FP8X4), z_scale[:], z_bf[u][:].rearrange("p v t -> p (v t)"))
             bank = psum.tile([P, VH], F32, name=f"out_bank{u}", tag=f"half_bank{u}")
             nc.tensor.matmul_mx(
                 bank[:],
@@ -169,49 +216,3 @@ def tile_picked_zfp_lin_p_kernel(
             else:
                 nc.vector.tensor_copy(result[:], bank[:])
             nc.sync.dma_start(out[:, cols], result[:])
-
-        lists = VH // 16
-        picked = [
-            [sbuf(f"picked{t}_{d}", [P, VH], F32, tag="late0" if (t, d) == (2, 1) else "") for d in range(2)] for t in range(PACK)
-        ]
-        for t in range(PACK):
-            for d in range(2):
-                nc.vector.tensor_copy(picked[t][d][:], h[t][:].indirect(pos_sb[d][:, :lists]))
-        z_bank = psum.tile([P, PACK, VH], F32, name="z_bank")
-        for pair in range(2):
-            turned = psum.tile([P, 2, 2, P], F32, name=f"turned{pair}")
-            gated = sbuf(f"gated{pair}", [P, 2, 2, P], F32)
-            for k in range(2):
-                for d in range(2):
-                    nc.tensor.transpose(turned[:, d, k, :], picked[2 * pair + k][d][:], identity[:])
-            for d in range(2):
-                nc.scalar.activation(gated[:, d], turned[:, d], COPY, scale=gate_cols[:, d : d + 1])
-            for k in range(2):
-                for d in range(2):
-                    nc.tensor.matmul(
-                        z_bank[:, 2 * pair + k, :],
-                        lhsT=gated[:, d, k, :],
-                        rhs=identity[:],
-                        is_transpose=True,
-                        start=(d == 0),
-                        stop=(d == 1),
-                    )
-        z_first = sbuf("z_first", [P, VH, PACK], BF16, tag="z_bf")
-        nc.scalar.copy(z_first[:], z_bank[:].rearrange("p t v -> p v t"))
-
-        nc.vector.quantize_mx(e_codes[:].bitcast(FP8X4), e_scale[:], e_bf[:].rearrange("p v j -> p (v j)"))
-        terms = [sbuf(f"terms{d}", [P, PACK, VH], F32, tag=f"late{d}") for d in range(2)]
-        for t in range(PACK):
-            for d in range(2):
-                nc.vector.tensor_tensor(
-                    terms[d][:, t, :], h[t][:].indirect(pos_sb[d][:, lists:]), gate_rows[:, d, :], ALU.mult
-                )
-        second_product(0, z_first)
-        z_second = sbuf("z_second", [P, VH, PACK], BF16, tag="z_bf")
-        nc.vector.tensor_tensor(
-            z_second[:].rearrange("p (c i) t -> p c t i", i=4),
-            terms[0][:].rearrange("p t (c i) -> p c t i", i=4),
-            terms[1][:].rearrange("p t (c i) -> p c t i", i=4),
-            ALU.add,
-        )
-        second_product(1, z_second)

@@ -20,8 +20,7 @@ RELU = mybir.ActivationFunctionType.Relu
 COPY = mybir.ActivationFunctionType.Copy
 VH = V // 2
 
-W_CHUNKS = 2
-W_COLS = H // W_CHUNKS
+X_FIRST = 640
 
 
 def tile_picked_zfp_lin_p_kernel(
@@ -46,7 +45,7 @@ def tile_picked_zfp_lin_p_kernel(
         pos_sb = [sbuf(f"pos_sb{d}", [P, V // 16], U16) for d in range(2)]
         xw_all = sbuf("xw_all", [P, T], I32)
         xs_all = sbuf("xs_all", [P, T], U8)
-        w1_raw = [sbuf(f"w1_raw{c}", [P, PACK, W_COLS], F32) for c in range(W_CHUNKS)]
+        w1_raw = [sbuf(f"w1_raw{c}", [P, 2, H], F32) for c in range(2)]
         gate_rows = [sbuf(f"gate_rows{d}", [P, V], F32, tag=f"gate_slot{d}") for d in range(2)]
         gate_cols = [sbuf(f"gate_cols{d}", [P, 2], F32) for d in range(2)]
         identity = sbuf("identity", [P, P], F32)
@@ -62,11 +61,12 @@ def tile_picked_zfp_lin_p_kernel(
         make_identity(nc, identity[:])
 
         nc.sync.dma_start(offs_sb[:], offs)
-        nc.sync.dma_start(xw_all[:], words_of(x_words))
+        nc.sync.dma_start(xw_all[:, :X_FIRST], words_of(x_words)[:, :X_FIRST])
         load_scales(nc.sync, xs_all, x_scales)
+        nc.sync.dma_start(xw_all[:, X_FIRST:], words_of(x_words)[:, X_FIRST:])
         w1_rows = w1.rearrange("(p j) c -> p j c", j=PACK)
-        for c in range(W_CHUNKS):
-            nc.sync.dma_start(w1_raw[c][:], w1_rows[:, :, c * W_COLS : (c + 1) * W_COLS])
+        for c in range(2):
+            nc.sync.dma_start(w1_raw[c][:], w1_rows[:, 2 * c : 2 * c + 2, :])
         nc.sync.dma_start(pos_sb[0][:], pos1)
         nc.sync.dma_start(pos_sb[1][:], pos2)
         nc.sync.dma_start(e_raw[:], eT.rearrange("(p j) v -> p j v", j=PACK))
@@ -80,28 +80,31 @@ def tile_picked_zfp_lin_p_kernel(
         load_scales(nc.sync, w3s, w3_scales)
         load_scales(nc.sync, w2s, w2_scales)
 
-        xw = sbuf("xw", [P, S], U32)
-        nc.vector.tensor_copy(xw[:], xw_all[:].bitcast(U32).indirect(offs_sb[:]))
         xs = sbuf("xs", [P, S], U8)
         nc.vector.tensor_copy(xs[:], xs_all[:].indirect(offs_sb[:]))
+        xw = sbuf("xw", [P, S], U32)
+        nc.vector.tensor_copy(xw[:], xw_all[:].bitcast(U32).indirect(offs_sb[:]))
 
-        w1_bf = sbuf("w1_bf", [P, PACK, P, PACK], BF16)
-        m_per = W_COLS // PACK
-        for c in range(W_CHUNKS):
-            dst = w1_bf[:].rearrange("p t m j -> p m t j")[:, c * m_per : (c + 1) * m_per]
-            src = w1_raw[c][:].rearrange("p j (m t) -> p m t j", t=PACK)
-            if c == 0:
-                nc.scalar.copy(dst, src)
-            else:
-                nc.vector.tensor_copy(dst[:, :, :2], src[:, :, :2])
-                nc.scalar.copy(dst[:, :, 2:], src[:, :, 2:])
+        w1_bf = [sbuf(f"w1_bf{g}", [P, 2, P, PACK], BF16) for g in range(2)]
 
-        w1_codes = [sbuf(f"w1_codes{t}", [P, P], U32, tag="late1" if t == PACK - 1 else "") for t in range(PACK)]
+        def round_w1(engine_copy, c, g, planes):
+            engine_copy(
+                w1_bf[g][:].rearrange("p t m j -> p m t j")[:, :, planes, 2 * c : 2 * c + 2],
+                w1_raw[c][:].rearrange("p j (m g t) -> p g m t j", g=2, t=2)[:, g, :, planes],
+            )
+
+        round_w1(nc.scalar.copy, 0, 0, slice(0, 2))
+        round_w1(nc.scalar.copy, 0, 1, slice(0, 2))
+        round_w1(nc.vector.tensor_copy, 1, 0, 0)
+        round_w1(nc.vector.tensor_copy, 1, 0, 1)
+        round_w1(nc.scalar.copy, 1, 1, slice(0, 2))
+
+        w1_codes = [sbuf(f"w1_codes{t}", [P, P], U32) for t in range(PACK)]
         w1_scale = [sbuf(f"w1_scale{t}", [P, P], U8) for t in range(PACK)]
 
         def quantize_w1(t):
             nc.vector.quantize_mx(
-                w1_codes[t][:].bitcast(FP8X4), w1_scale[t][:], w1_bf[:, t].rearrange("p m j -> p (m j)")
+                w1_codes[t][:].bitcast(FP8X4), w1_scale[t][:], w1_bf[t // 2][:, t % 2].rearrange("p m j -> p (m j)")
             )
 
         half = S // 2
@@ -123,23 +126,18 @@ def tile_picked_zfp_lin_p_kernel(
         h0_banks = [psum.tile([P, half], F32, name=f"h0_bank{u}", tag=f"half_bank{u}") for u in range(2)]
         for u in range(2):
             first_product(0, h0_banks[u][:], slice(u * half, (u + 1) * half))
-        nc.vector.tensor_scalar(h[0][:, :half], h0_banks[0][:], 0.0, None, ALU.max)
-        nc.scalar.activation(h[0][:, half:], h0_banks[1][:], RELU)
+        for u in range(2):
+            nc.scalar.activation(h[0][:, u * half : (u + 1) * half], h0_banks[u][:], RELU)
         for t in range(1, PACK):
             bank = psum.tile([P, S], F32, name=f"h_bank{t}", tag=f"h_slot{t}")
             first_product(t, bank[:], slice(0, S))
             nc.scalar.activation(h[t][:], bank[:], RELU)
 
-        e_bf = sbuf("e_bf", [P, V, PACK], BF16, tag="late1")
-
-        def round_e(u):
-            cols = slice(u * VH, (u + 1) * VH)
-            nc.scalar.copy(
-                e_bf[:, cols].rearrange("p (c i) j -> p c j i", i=4),
-                e_raw[:, :, cols].rearrange("p j (c i) -> p c j i", i=4),
-            )
-
-        round_e(0)
+        e_bf = sbuf("e_bf", [P, V, PACK], BF16)
+        nc.vector.tensor_copy(
+            e_bf[:].rearrange("p (c i) j -> p c j i", i=4),
+            e_raw[:].rearrange("p j (c i) -> p c j i", i=4),
+        )
         z_bf = [sbuf(f"z_bf{u}", [P, VH, PACK], BF16) for u in range(2)]
 
         picked = [[sbuf(f"picked{t}_{d}", [P, V], F32) for d in range(2)] for t in range(2)]
@@ -155,7 +153,6 @@ def tile_picked_zfp_lin_p_kernel(
                     nc.tensor.transpose(turned[:, u, t, :], picked[t][d][:, u * VH : (u + 1) * VH], identity[:])
             for u in range(2):
                 nc.scalar.activation(gated[d][:, u], turned[:, u], COPY, scale=gate_cols[d][:, u : u + 1])
-        round_e(1)
         for u in range(2):
             z_bank = psum.tile([P, 2, VH], F32, name=f"z_bank{u}", tag=f"h_slot{u + 1}")
             for t in range(2):

@@ -46,7 +46,7 @@ def tile_picked_zfp_lin_p_kernel(
         xw_all = sbuf("xw_all", [P, T], I32)
         xs_all = sbuf("xs_all", [P, T], U8)
         w1_raw = [sbuf(f"w1_raw{c}", [P, 2, H], F32) for c in range(2)]
-        gate_rows = [sbuf(f"gate_rows{d}", [P, V], F32, tag=f"gate_slot{d}") for d in range(2)]
+        gate_rows = [sbuf(f"gate_rows{d}", [P, V], F32) for d in range(2)]
         gate_cols = [sbuf(f"gate_cols{d}", [P, 2], F32) for d in range(2)]
         identity = sbuf("identity", [P, P], F32)
         e_raw = sbuf("e_raw", [P, PACK, V], F32)
@@ -68,8 +68,8 @@ def tile_picked_zfp_lin_p_kernel(
         for c in range(2):
             nc.sync.dma_start(w1_raw[c][:], w1_rows[:, 2 * c : 2 * c + 2, :])
         nc.sync.dma_start(pos_sb[0][:], pos1)
-        nc.sync.dma_start(pos_sb[1][:], pos2)
         nc.sync.dma_start(e_raw[:], eT.rearrange("(p j) v -> p j v", j=PACK))
+        nc.sync.dma_start(pos_sb[1][:], pos2)
         with nc.allow_non_contiguous_dma(reason="one gate value a partition"):
             for d in range(2):
                 nc.sync.dma_start(gate_cols[d][:], gate[d, 0, :].rearrange("(u v) -> v u", u=2))
@@ -99,22 +99,34 @@ def tile_picked_zfp_lin_p_kernel(
         round_w1(nc.vector.tensor_copy, 1, 0, 1)
         round_w1(nc.scalar.copy, 1, 1, slice(0, 2))
 
-        w1_codes = [sbuf(f"w1_codes{t}", [P, P], U32) for t in range(PACK)]
+        late_codes = sbuf("late_codes", [P, 2, P], U32)
+        w1_codes = [sbuf(f"w1_codes{t}", [P, P], U32)[:] for t in range(2)] + [late_codes[:, t] for t in range(2)]
         w1_scale = [sbuf(f"w1_scale{t}", [P, P], U8) for t in range(PACK)]
 
         def quantize_w1(t):
             nc.vector.quantize_mx(
-                w1_codes[t][:].bitcast(FP8X4), w1_scale[t][:], w1_bf[t // 2][:, t % 2].rearrange("p m j -> p (m j)")
+                w1_codes[t].bitcast(FP8X4), w1_scale[t][:], w1_bf[t // 2][:, t % 2].rearrange("p m j -> p (m j)")
             )
 
         half = S // 2
-        for t in range(PACK):
+        for t in range(2):
             quantize_w1(t)
+        e_bf = sbuf("e_bf", [P, V, PACK], BF16)
+        nc.vector.tensor_copy(
+            e_bf[:].rearrange("p (c i) j -> p c j i", i=4),
+            e_raw[:].rearrange("p j (c i) -> p c j i", i=4),
+        )
+        for t in range(2, PACK):
+            quantize_w1(t)
+
+        e_codes = sbuf("e_codes", [P, V], U32)
+        e_scale = sbuf("e_scale", [P, V], U8)
+        nc.vector.quantize_mx(e_codes[:].bitcast(FP8X4), e_scale[:], e_bf[:].rearrange("p v j -> p (v j)"))
 
         def first_product(t, bank, cols):
             nc.tensor.matmul_mx(
                 bank,
-                lhsT=w1_codes[t][:].bitcast(FP8X4),
+                lhsT=w1_codes[t].bitcast(FP8X4),
                 lhsT_scale=w1_scale[t][:],
                 rhs=xw[:, cols].bitcast(FP8X4),
                 rhs_scale=xs[:, cols],
@@ -133,48 +145,44 @@ def tile_picked_zfp_lin_p_kernel(
             first_product(t, bank[:], slice(0, S))
             nc.scalar.activation(h[t][:], bank[:], RELU)
 
-        e_bf = sbuf("e_bf", [P, V, PACK], BF16)
-        nc.vector.tensor_copy(
-            e_bf[:].rearrange("p (c i) j -> p c j i", i=4),
-            e_raw[:].rearrange("p j (c i) -> p c j i", i=4),
-        )
         z_bf = [sbuf(f"z_bf{u}", [P, VH, PACK], BF16) for u in range(2)]
 
         picked = [[sbuf(f"picked{t}_{d}", [P, V], F32) for d in range(2)] for t in range(2)]
         for t in range(2):
             for d in range(2):
                 nc.vector.tensor_copy(picked[t][d][:], h[t][:].indirect(pos_sb[d][:]))
-        gated = []
-        for d in range(2):
-            turned = psum.tile([P, 2, 2, P], F32, name=f"turned{d}")
-            gated.append(sbuf(f"gated{d}", [P, 2, 2, P], F32))
-            for t in range(2):
+        z_banks = [psum.tile([P, 2, VH], F32, name=f"z_bank{u}", tag=f"h_slot{u + 1}") for u in range(2)]
+        for t in range(2):
+            turned = psum.tile([P, 2, 2, P], F32, name=f"turned{t}")
+            for d in range(2):
                 for u in range(2):
-                    nc.tensor.transpose(turned[:, u, t, :], picked[t][d][:, u * VH : (u + 1) * VH], identity[:])
+                    nc.tensor.transpose(turned[:, u, d, :], picked[t][d][:, u * VH : (u + 1) * VH], identity[:])
             for u in range(2):
-                nc.scalar.activation(gated[d][:, u], turned[:, u], COPY, scale=gate_cols[d][:, u : u + 1])
-        for u in range(2):
-            z_bank = psum.tile([P, 2, VH], F32, name=f"z_bank{u}", tag=f"h_slot{u + 1}")
-            for t in range(2):
+                gated = [sbuf(f"gated{t}_{u}_{d}", [P, P], F32) for d in range(2)]
+                for d in range(2):
+                    nc.scalar.activation(gated[d][:], turned[:, u, d, :], COPY, scale=gate_cols[d][:, u : u + 1])
                 for d in range(2):
                     nc.tensor.matmul(
-                        z_bank[:, t, :],
-                        lhsT=gated[d][:, u, t, :],
+                        z_banks[u][:, t, :],
+                        lhsT=gated[d][:],
                         rhs=identity[:],
                         is_transpose=True,
                         start=(d == 0),
                         stop=(d == 1),
                     )
-            nc.scalar.copy(z_bf[u][:, :, 0:2], z_bank[:].rearrange("p t v -> p v t"))
+        for u in range(2):
+            nc.scalar.copy(z_bf[u][:, :, 0:2], z_banks[u][:].rearrange("p t v -> p v t"))
 
+        whole = [(slice(0, V), slice(0, V // 16))]
+        halves = [(slice(u * VH, (u + 1) * VH), slice(u * VH // 16, (u + 1) * VH // 16)) for u in range(2)]
         terms = [sbuf(f"terms{d}", [P, 2, V], F32) for d in range(2)]
         for t in range(2):
             for d in range(2):
-                nc.vector.tensor_tensor(terms[d][:, t, :], h[2 + t][:].indirect(pos_sb[d][:]), gate_rows[d][:], ALU.mult)
+                for cols, lists in halves if (t, d) == (1, 1) else whole:
+                    nc.vector.tensor_tensor(
+                        terms[d][:, t, cols], h[2 + t][:].indirect(pos_sb[d][:, lists]), gate_rows[d][:, cols], ALU.mult
+                    )
 
-        e_codes = sbuf("e_codes", [P, V], U32, tag="gate_slot0")
-        e_scale = sbuf("e_scale", [P, V], U8)
-        nc.vector.quantize_mx(e_codes[:].bitcast(FP8X4), e_scale[:], e_bf[:].rearrange("p v j -> p (v j)"))
         for u in range(2):
             cols = slice(u * VH, (u + 1) * VH)
             nc.vector.tensor_tensor(

@@ -67,8 +67,8 @@ def tile_picked_zfp_lin_p_kernel(
         w1_rows = w1.rearrange("(p j) c -> p j c", j=PACK)
         for c in range(2):
             nc.sync.dma_start(w1_raw[c][:], w1_rows[:, 2 * c : 2 * c + 2, :])
-        nc.sync.dma_start(pos_sb[0][:], pos1)
         nc.sync.dma_start(e_raw[:], eT.rearrange("(p j) v -> p j v", j=PACK))
+        nc.sync.dma_start(pos_sb[0][:], pos1)
         nc.sync.dma_start(pos_sb[1][:], pos2)
         with nc.allow_non_contiguous_dma(reason="one gate value a partition"):
             for d in range(2):
@@ -101,11 +101,12 @@ def tile_picked_zfp_lin_p_kernel(
 
         late_codes = sbuf("late_codes", [P, 2, P], U32)
         w1_codes = [sbuf(f"w1_codes{t}", [P, P], U32)[:] for t in range(2)] + [late_codes[:, t] for t in range(2)]
-        w1_scale = [sbuf(f"w1_scale{t}", [P, P], U8) for t in range(PACK)]
+        late_scale = sbuf("late_scale", [P, 2, P], U8)
+        w1_scale = [sbuf(f"w1_scale{t}", [P, P], U8)[:] for t in range(2)] + [late_scale[:, t] for t in range(2)]
 
         def quantize_w1(t):
             nc.vector.quantize_mx(
-                w1_codes[t].bitcast(FP8X4), w1_scale[t][:], w1_bf[t // 2][:, t % 2].rearrange("p m j -> p (m j)")
+                w1_codes[t].bitcast(FP8X4), w1_scale[t], w1_bf[t // 2][:, t % 2].rearrange("p m j -> p (m j)")
             )
 
         half = S // 2
@@ -116,8 +117,11 @@ def tile_picked_zfp_lin_p_kernel(
             e_bf[:].rearrange("p (c i) j -> p c j i", i=4),
             e_raw[:].rearrange("p j (c i) -> p c j i", i=4),
         )
-        for t in range(2, PACK):
-            quantize_w1(t)
+        nc.vector.quantize_mx(
+            late_codes[:].rearrange("p t m -> p (t m)").bitcast(FP8X4),
+            late_scale[:].rearrange("p t m -> p (t m)"),
+            w1_bf[1][:].rearrange("p t m j -> p (t m j)"),
+        )
 
         e_codes = sbuf("e_codes", [P, V], U32)
         e_scale = sbuf("e_scale", [P, V], U8)
@@ -127,7 +131,7 @@ def tile_picked_zfp_lin_p_kernel(
             nc.tensor.matmul_mx(
                 bank,
                 lhsT=w1_codes[t].bitcast(FP8X4),
-                lhsT_scale=w1_scale[t][:],
+                lhsT_scale=w1_scale[t],
                 rhs=xw[:, cols].bitcast(FP8X4),
                 rhs_scale=xs[:, cols],
                 start=True,

@@ -19,6 +19,7 @@ ALU = mybir.AluOpType
 RELU = mybir.ActivationFunctionType.Relu
 COPY = mybir.ActivationFunctionType.Copy
 VH = V // 2
+MH = P // 2
 
 X_FIRST = 640
 
@@ -45,7 +46,7 @@ def tile_picked_zfp_lin_p_kernel(
         pos_sb = [sbuf(f"pos_sb{d}", [P, V // 16], U16) for d in range(2)]
         xw_all = sbuf("xw_all", [P, T], I32)
         xs_all = sbuf("xs_all", [P, T], U8)
-        w1_raw = [sbuf(f"w1_raw{c}", [P, 2, H], F32) for c in range(2)]
+        w1_raw = [sbuf(f"w1_raw{c}", [P, PACK, H // 2], F32, tag=f"w1_slot{c}") for c in range(2)]
         gate_rows = [sbuf(f"gate_rows{d}", [P, V], F32) for d in range(2)]
         gate_cols = [sbuf(f"gate_cols{d}", [P, 2], F32) for d in range(2)]
         identity = sbuf("identity", [P, P], F32)
@@ -66,7 +67,7 @@ def tile_picked_zfp_lin_p_kernel(
         nc.sync.dma_start(xw_all[:, X_FIRST:], words_of(x_words)[:, X_FIRST:])
         w1_rows = w1.rearrange("(p j) c -> p j c", j=PACK)
         for c in range(2):
-            nc.sync.dma_start(w1_raw[c][:], w1_rows[:, 2 * c : 2 * c + 2, :])
+            nc.sync.dma_start(w1_raw[c][:], w1_rows[:, :, c * H // 2 : (c + 1) * H // 2])
         nc.sync.dma_start(e_raw[:], eT.rearrange("(p j) v -> p j v", j=PACK))
         nc.sync.dma_start(pos_sb[0][:], pos1)
         nc.sync.dma_start(pos_sb[1][:], pos2)
@@ -85,47 +86,46 @@ def tile_picked_zfp_lin_p_kernel(
         xw = sbuf("xw", [P, S], U32)
         nc.vector.tensor_copy(xw[:], xw_all[:].bitcast(U32).indirect(offs_sb[:]))
 
-        w1_bf = [sbuf(f"w1_bf{g}", [P, 2, P, PACK], BF16) for g in range(2)]
+        early_bf = [sbuf(f"early_bf{c}", [P, 2, MH, PACK], BF16, tag="early_bf") for c in range(2)]
+        late_bf = sbuf("late_bf", [P, 2, P, PACK], BF16)
 
-        def round_w1(engine_copy, c, g, planes):
+        def round_w1(engine_copy, target, c, g, rows):
             engine_copy(
-                w1_bf[g][:].rearrange("p t m j -> p m t j")[:, :, planes, 2 * c : 2 * c + 2],
-                w1_raw[c][:].rearrange("p j (m g t) -> p g m t j", g=2, t=2)[:, g, :, planes],
+                target.rearrange("p t m j -> p m t j")[:, rows],
+                w1_raw[c][:].rearrange("p j (m g t) -> p g m t j", g=2, t=2)[:, g, rows],
             )
 
-        round_w1(nc.scalar.copy, 0, 0, slice(0, 2))
-        round_w1(nc.scalar.copy, 0, 1, slice(0, 2))
-        round_w1(nc.vector.tensor_copy, 1, 0, 0)
-        round_w1(nc.vector.tensor_copy, 1, 0, 1)
-        round_w1(nc.scalar.copy, 1, 1, slice(0, 2))
-
         late_codes = sbuf("late_codes", [P, 2, P], U32)
-        w1_codes = [sbuf(f"w1_codes{t}", [P, P], U32)[:] for t in range(2)] + [late_codes[:, t] for t in range(2)]
+        w1_codes = [sbuf(f"w1_codes{t}", [P, P], U32, tag=f"codes{t}")[:] for t in range(2)] + [late_codes[:, t] for t in range(2)]
         late_scale = sbuf("late_scale", [P, 2, P], U8)
         w1_scale = [sbuf(f"w1_scale{t}", [P, P], U8)[:] for t in range(2)] + [late_scale[:, t] for t in range(2)]
 
-        def quantize_w1(t):
+        def quantize_early(c):
             nc.vector.quantize_mx(
-                w1_codes[t].bitcast(FP8X4), w1_scale[t], w1_bf[t // 2][:, t % 2].rearrange("p m j -> p (m j)")
+                w1_codes[c].bitcast(FP8X4), w1_scale[c], early_bf[c][:].rearrange("p t m j -> p (t m j)")
             )
 
         half = S // 2
-        for t in range(2):
-            quantize_w1(t)
-        e_bf = sbuf("e_bf", [P, V, PACK], BF16)
-        nc.vector.tensor_copy(
-            e_bf[:].rearrange("p (c i) j -> p c j i", i=4),
-            e_raw[:].rearrange("p j (c i) -> p c j i", i=4),
-        )
+        round_w1(nc.scalar.copy, early_bf[0][:], 0, 0, slice(0, MH))
+        round_w1(nc.scalar.copy, late_bf[:, :, :MH], 0, 1, slice(0, MH))
+        round_w1(nc.scalar.copy, late_bf[:, :, MH:], 1, 1, slice(0, MH))
+        quantize_early(0)
+        round_w1(nc.vector.tensor_copy, early_bf[1][:], 1, 0, slice(0, MH))
+        quantize_early(1)
         nc.vector.quantize_mx(
             late_codes[:].rearrange("p t m -> p (t m)").bitcast(FP8X4),
             late_scale[:].rearrange("p t m -> p (t m)"),
-            w1_bf[1][:].rearrange("p t m j -> p (t m j)"),
+            late_bf[:].rearrange("p t m j -> p (t m j)"),
         )
+        e_bf = [sbuf(f"e_bf{u}", [P, VH, PACK], BF16, tag=("w1_slot1", "codes1")[u]) for u in range(2)]
 
-        e_codes = sbuf("e_codes", [P, V], U32)
-        e_scale = sbuf("e_scale", [P, V], U8)
-        nc.vector.quantize_mx(e_codes[:].bitcast(FP8X4), e_scale[:], e_bf[:].rearrange("p v j -> p (v j)"))
+        def round_e(engine_copy, u):
+            engine_copy(
+                e_bf[u][:].rearrange("p (c i) j -> p c j i", i=4),
+                e_raw[:, :, u * VH : (u + 1) * VH].rearrange("p j (c i) -> p c j i", i=4),
+            )
+
+        round_e(nc.vector.tensor_copy, 0)
 
         def first_product(t, bank, cols):
             nc.tensor.matmul_mx(
@@ -149,26 +149,41 @@ def tile_picked_zfp_lin_p_kernel(
             first_product(t, bank[:], slice(0, S))
             nc.scalar.activation(h[t][:], bank[:], RELU)
 
+        round_e(nc.scalar.copy, 1)
         z_bf = [sbuf(f"z_bf{u}", [P, VH, PACK], BF16) for u in range(2)]
 
-        picked = [[sbuf(f"picked{t}_{d}", [P, V], F32) for d in range(2)] for t in range(2)]
-        for t in range(2):
+        picked = [[sbuf(f"picked{c}_{d}", [P, V], F32) for d in range(2)] for c in range(2)]
+        for c in range(2):
             for d in range(2):
-                nc.vector.tensor_copy(picked[t][d][:], h[t][:].indirect(pos_sb[d][:]))
+                nc.vector.tensor_copy(picked[c][d][:], h[c][:].indirect(pos_sb[d][:]))
+        e_codes = sbuf("e_codes", [P, V], U32)
+        e_scale = sbuf("e_scale", [P, V], U8)
+        for u in range(2):
+            cols = slice(u * VH, (u + 1) * VH)
+            nc.vector.quantize_mx(
+                e_codes[:, cols].bitcast(FP8X4), e_scale[:, cols], e_bf[u][:].rearrange("p v j -> p (v j)")
+            )
+
         z_banks = [psum.tile([P, 2, VH], F32, name=f"z_bank{u}", tag=f"h_slot{u + 1}") for u in range(2)]
-        for t in range(2):
-            turned = psum.tile([P, 2, 2, P], F32, name=f"turned{t}")
+        gated = [[sbuf(f"gated{u}_{d}", [P, 2, P], F32) for d in range(2)] for u in range(2)]
+        for c in range(2):
             for d in range(2):
+                turned = psum.tile([P, 2, P], F32, name=f"turned{c}_{d}", tag=f"turn_slot{(2 * c + d) % 3}")
                 for u in range(2):
-                    nc.tensor.transpose(turned[:, u, d, :], picked[t][d][:, u * VH : (u + 1) * VH], identity[:])
-            for u in range(2):
-                gated = [sbuf(f"gated{t}_{u}_{d}", [P, P], F32) for d in range(2)]
-                for d in range(2):
-                    nc.scalar.activation(gated[d][:], turned[:, u, d, :], COPY, scale=gate_cols[d][:, u : u + 1])
+                    nc.tensor.transpose(turned[:, u, :], picked[c][d][:, u * VH : (u + 1) * VH], identity[:])
+                for u in range(2):
+                    nc.scalar.activation(
+                        gated[u][d][:, :, c * MH : (c + 1) * MH],
+                        turned[:, u, :].rearrange("p (t m) -> p t m", t=2),
+                        COPY,
+                        scale=gate_cols[d][:, u : u + 1],
+                    )
+        for u in range(2):
+            for t in range(2):
                 for d in range(2):
                     nc.tensor.matmul(
                         z_banks[u][:, t, :],
-                        lhsT=gated[d][:],
+                        lhsT=gated[u][d][:, t, :],
                         rhs=identity[:],
                         is_transpose=True,
                         start=(d == 0),

@@ -46,7 +46,7 @@ def tile_picked_zfp_lin_p_kernel(
         pos_sb = [sbuf(f"pos_sb{d}", [P, V // 16], U16) for d in range(2)]
         xw_all = sbuf("xw_all", [P, T], I32)
         xs_all = sbuf("xs_all", [P, T], U8)
-        w1_raw = [sbuf(f"w1_raw{c}", [P, PACK, H // 2], F32, tag=f"w1_slot{c}") for c in range(2)]
+        w1_raw = [sbuf(f"w1_raw{c}", [P, PACK, H // 2], F32) for c in range(2)]
         gate_rows = [sbuf(f"gate_rows{d}", [P, V], F32) for d in range(2)]
         gate_cols = [sbuf(f"gate_cols{d}", [P, 2], F32) for d in range(2)]
         identity = sbuf("identity", [P, P], F32)
@@ -68,8 +68,8 @@ def tile_picked_zfp_lin_p_kernel(
         w1_rows = w1.rearrange("(p j) c -> p j c", j=PACK)
         for c in range(2):
             nc.sync.dma_start(w1_raw[c][:], w1_rows[:, :, c * H // 2 : (c + 1) * H // 2])
-        nc.sync.dma_start(e_raw[:], eT.rearrange("(p j) v -> p j v", j=PACK))
         nc.sync.dma_start(pos_sb[0][:], pos1)
+        nc.sync.dma_start(e_raw[:], eT.rearrange("(p j) v -> p j v", j=PACK))
         nc.sync.dma_start(pos_sb[1][:], pos2)
         with nc.allow_non_contiguous_dma(reason="one gate value a partition"):
             for d in range(2):
@@ -86,8 +86,10 @@ def tile_picked_zfp_lin_p_kernel(
         xw = sbuf("xw", [P, S], U32)
         nc.vector.tensor_copy(xw[:], xw_all[:].bitcast(U32).indirect(offs_sb[:]))
 
-        early_bf = [sbuf(f"early_bf{c}", [P, 2, MH, PACK], BF16, tag="early_bf") for c in range(2)]
-        late_bf = sbuf("late_bf", [P, 2, P, PACK], BF16)
+        w1_bf = sbuf("w1_bf", [P, 3 * P, PACK], BF16)
+        late_bf = w1_bf[:, : 2 * P].rearrange("p (t m) j -> p t m j", t=2)
+        second_bf = w1_bf[:, 2 * P :].rearrange("p (t m) j -> p t m j", t=2)
+        first_bf = w1_bf[:, 2 * P - MH : 3 * P - MH].rearrange("p (t m) j -> p t m j", t=2)
 
         def round_w1(engine_copy, target, c, g, rows):
             engine_copy(
@@ -100,32 +102,38 @@ def tile_picked_zfp_lin_p_kernel(
         late_scale = sbuf("late_scale", [P, 2, P], U8)
         w1_scale = [sbuf(f"w1_scale{t}", [P, P], U8)[:] for t in range(2)] + [late_scale[:, t] for t in range(2)]
 
-        def quantize_early(c):
-            nc.vector.quantize_mx(
-                w1_codes[c].bitcast(FP8X4), w1_scale[c], early_bf[c][:].rearrange("p t m j -> p (t m j)")
-            )
+        def quantize_early(c, rounded):
+            nc.vector.quantize_mx(w1_codes[c].bitcast(FP8X4), w1_scale[c], rounded.rearrange("p t m j -> p (t m j)"))
 
         half = S // 2
-        round_w1(nc.scalar.copy, early_bf[0][:], 0, 0, slice(0, MH))
+        round_w1(nc.scalar.copy, first_bf, 0, 0, slice(0, MH))
+        quantize_early(0, first_bf)
         round_w1(nc.scalar.copy, late_bf[:, :, :MH], 0, 1, slice(0, MH))
-        round_w1(nc.scalar.copy, late_bf[:, :, MH:], 1, 1, slice(0, MH))
-        quantize_early(0)
-        round_w1(nc.vector.tensor_copy, early_bf[1][:], 1, 0, slice(0, MH))
-        quantize_early(1)
+        round_w1(nc.vector.tensor_copy, second_bf, 1, 0, slice(0, MH))
+        round_w1(nc.vector.tensor_copy, late_bf[:, :, MH:], 1, 1, slice(0, MH))
+        quantize_early(1, second_bf)
         nc.vector.quantize_mx(
             late_codes[:].rearrange("p t m -> p (t m)").bitcast(FP8X4),
             late_scale[:].rearrange("p t m -> p (t m)"),
-            late_bf[:].rearrange("p t m j -> p (t m j)"),
+            late_bf.rearrange("p t m j -> p (t m j)"),
         )
-        e_bf = [sbuf(f"e_bf{u}", [P, VH, PACK], BF16, tag=("w1_slot1", "codes1")[u]) for u in range(2)]
 
-        def round_e(engine_copy, u):
-            engine_copy(
-                e_bf[u][:].rearrange("p (c i) j -> p c j i", i=4),
+        def round_e(u, slot):
+            rounded = sbuf(f"e_bf{u}", [P, VH, PACK], BF16, tag=slot)
+            nc.scalar.copy(
+                rounded[:].rearrange("p (c i) j -> p c j i", i=4),
                 e_raw[:, :, u * VH : (u + 1) * VH].rearrange("p j (c i) -> p c j i", i=4),
             )
+            return rounded
 
-        round_e(nc.vector.tensor_copy, 0)
+        e_codes = sbuf("e_codes", [P, V], U32)
+        e_scale = sbuf("e_scale", [P, V], U8)
+
+        def quantize_e(u, rounded):
+            cols = slice(u * VH, (u + 1) * VH)
+            nc.vector.quantize_mx(
+                e_codes[:, cols].bitcast(FP8X4), e_scale[:, cols], rounded[:].rearrange("p v j -> p (v j)")
+            )
 
         def first_product(t, bank, cols):
             nc.tensor.matmul_mx(
@@ -149,20 +157,14 @@ def tile_picked_zfp_lin_p_kernel(
             first_product(t, bank[:], slice(0, S))
             nc.scalar.activation(h[t][:], bank[:], RELU)
 
-        round_e(nc.scalar.copy, 1)
+        e_first = round_e(0, "codes0")
         z_bf = [sbuf(f"z_bf{u}", [P, VH, PACK], BF16) for u in range(2)]
 
-        picked = [[sbuf(f"picked{c}_{d}", [P, V], F32) for d in range(2)] for c in range(2)]
+        picked = [[sbuf(f"picked{c}_{d}", [P, V], F32, tag=f"picked{c}_{d}") for d in range(2)] for c in range(2)]
         for c in range(2):
             for d in range(2):
                 nc.vector.tensor_copy(picked[c][d][:], h[c][:].indirect(pos_sb[d][:]))
-        e_codes = sbuf("e_codes", [P, V], U32)
-        e_scale = sbuf("e_scale", [P, V], U8)
-        for u in range(2):
-            cols = slice(u * VH, (u + 1) * VH)
-            nc.vector.quantize_mx(
-                e_codes[:, cols].bitcast(FP8X4), e_scale[:, cols], e_bf[u][:].rearrange("p v j -> p (v j)")
-            )
+        quantize_e(0, e_first)
 
         z_banks = [psum.tile([P, 2, VH], F32, name=f"z_bank{u}", tag=f"h_slot{u + 1}") for u in range(2)]
         gated = [[sbuf(f"gated{u}_{d}", [P, 2, P], F32) for d in range(2)] for u in range(2)]
@@ -178,6 +180,7 @@ def tile_picked_zfp_lin_p_kernel(
                         COPY,
                         scale=gate_cols[d][:, u : u + 1],
                     )
+        e_second = round_e(1, "picked1_1")
         for u in range(2):
             for t in range(2):
                 for d in range(2):
@@ -210,6 +213,7 @@ def tile_picked_zfp_lin_p_kernel(
                 terms[1][:, :, cols].rearrange("p t v -> p v t"),
                 ALU.add,
             )
+        quantize_e(1, e_second)
         for u in range(2):
             cols = slice(u * VH, (u + 1) * VH)
             z_codes = sbuf(f"z_codes{u}", [P, VH], U32)

@@ -21,7 +21,7 @@ COPY = mybir.ActivationFunctionType.Copy
 VH = V // 2
 MH = P // 2
 
-X_FIRST = 640
+X_FIRST = 384
 
 
 def tile_picked_zfp_lin_p_kernel(
@@ -38,8 +38,8 @@ def tile_picked_zfp_lin_p_kernel(
         def words_of(packed):
             return packed[0].rearrange("p c r -> p (c r)").bitcast(I32)
 
-        def load_scales(queue, plane, scales):
-            for q in range(4):
+        def load_scales(queue, plane, scales, quadrants=range(4)):
+            for q in quadrants:
                 queue.dma_start(plane[32 * q : 32 * q + 4, :].bitcast(I32), scales[0, 4 * q : 4 * q + 4, :].bitcast(I32))
 
         offs_sb = sbuf("offs_sb", [P, S // 16], U16)
@@ -63,11 +63,13 @@ def tile_picked_zfp_lin_p_kernel(
 
         nc.sync.dma_start(offs_sb[:], offs)
         nc.sync.dma_start(xw_all[:, :X_FIRST], words_of(x_words)[:, :X_FIRST])
-        load_scales(nc.sync, xs_all, x_scales)
+        load_scales(nc.scalar, xs_all, x_scales, range(2))
+        load_scales(nc.sync, xs_all, x_scales, range(2, 4))
         nc.sync.dma_start(xw_all[:, X_FIRST:], words_of(x_words)[:, X_FIRST:])
         w1_rows = w1.rearrange("(p j) c -> p j c", j=PACK)
-        for c in range(2):
-            nc.sync.dma_start(w1_raw[c][:], w1_rows[:, :, c * H // 2 : (c + 1) * H // 2])
+        for pair in range(2):
+            nc.sync.dma_start(w1_raw[0][:, 2 * pair : 2 * pair + 2], w1_rows[:, 2 * pair : 2 * pair + 2, : H // 2])
+        nc.sync.dma_start(w1_raw[1][:], w1_rows[:, :, H // 2 :])
         nc.sync.dma_start(pos_sb[0][:], pos1)
         nc.sync.dma_start(e_raw[:], eT.rearrange("(p j) v -> p j v", j=PACK))
         nc.sync.dma_start(pos_sb[1][:], pos2)
@@ -91,10 +93,10 @@ def tile_picked_zfp_lin_p_kernel(
         second_bf = w1_bf[:, 2 * P :].rearrange("p (t m) j -> p t m j", t=2)
         first_bf = w1_bf[:, 2 * P - MH : 3 * P - MH].rearrange("p (t m) j -> p t m j", t=2)
 
-        def round_w1(engine_copy, target, c, g, rows):
+        def round_w1(engine_copy, target, c, g, rows, slots=slice(0, PACK)):
             engine_copy(
-                target.rearrange("p t m j -> p m t j")[:, rows],
-                w1_raw[c][:].rearrange("p j (m g t) -> p g m t j", g=2, t=2)[:, g, rows],
+                target.rearrange("p t m j -> p m t j")[:, rows, :, slots],
+                w1_raw[c][:].rearrange("p j (m g t) -> p g m t j", g=2, t=2)[:, g, rows, :, slots],
             )
 
         late_codes = sbuf("late_codes", [P, 2, P], U32)
@@ -106,7 +108,8 @@ def tile_picked_zfp_lin_p_kernel(
             nc.vector.quantize_mx(w1_codes[c].bitcast(FP8X4), w1_scale[c], rounded.rearrange("p t m j -> p (t m j)"))
 
         half = S // 2
-        round_w1(nc.scalar.copy, first_bf, 0, 0, slice(0, MH))
+        for pair in range(2):
+            round_w1(nc.scalar.copy, first_bf, 0, 0, slice(0, MH), slice(2 * pair, 2 * pair + 2))
         quantize_early(0, first_bf)
         round_w1(nc.scalar.copy, late_bf[:, :, :MH], 0, 1, slice(0, MH))
         round_w1(nc.vector.tensor_copy, second_bf, 1, 0, slice(0, MH))

@@ -67,9 +67,10 @@ def tile_picked_zfp_lin_p_kernel(
         load_scales(nc.sync, xs_all, x_scales, range(2, 4))
         nc.sync.dma_start(xw_all[:, X_FIRST:], words_of(x_words)[:, X_FIRST:])
         w1_rows = w1.rearrange("(p j) c -> p j c", j=PACK)
-        for pair in range(2):
-            nc.sync.dma_start(w1_raw[0][:, 2 * pair : 2 * pair + 2], w1_rows[:, 2 * pair : 2 * pair + 2, : H // 2])
-        nc.sync.dma_start(w1_raw[1][:], w1_rows[:, :, H // 2 :])
+        pairs = [slice(0, 2), slice(2, 4)]
+        for c in range(2):
+            for pair in pairs:
+                nc.sync.dma_start(w1_raw[c][:, pair], w1_rows[:, pair, c * H // 2 : (c + 1) * H // 2])
         nc.sync.dma_start(pos_sb[0][:], pos1)
         nc.sync.dma_start(e_raw[:], eT.rearrange("(p j) v -> p j v", j=PACK))
         nc.sync.dma_start(pos_sb[1][:], pos2)
@@ -112,8 +113,10 @@ def tile_picked_zfp_lin_p_kernel(
             round_w1(nc.scalar.copy, first_bf, 0, 0, slice(0, MH), slice(2 * pair, 2 * pair + 2))
         quantize_early(0, first_bf)
         round_w1(nc.scalar.copy, late_bf[:, :, :MH], 0, 1, slice(0, MH))
-        round_w1(nc.vector.tensor_copy, second_bf, 1, 0, slice(0, MH))
-        round_w1(nc.vector.tensor_copy, late_bf[:, :, MH:], 1, 1, slice(0, MH))
+        round_w1(nc.scalar.copy, late_bf[:, :, MH:], 1, 1, slice(0, MH), pairs[0])
+        for pair in pairs:
+            round_w1(nc.vector.tensor_copy, second_bf, 1, 0, slice(0, MH), pair)
+        round_w1(nc.vector.tensor_copy, late_bf[:, :, MH:], 1, 1, slice(0, MH), pairs[1])
         quantize_early(1, second_bf)
         nc.vector.quantize_mx(
             late_codes[:].rearrange("p t m -> p (t m)").bitcast(FP8X4),

@@ -158,7 +158,12 @@ def tile_picked_zfp_lin_p_kernel(
             first_product(0, h0_banks[u][:], slice(u * half, (u + 1) * half))
         for u in range(2):
             nc.scalar.activation(h[0][:, u * half : (u + 1) * half], h0_banks[u][:], RELU)
-        for t in range(1, PACK):
+        for u, tag in enumerate(("h_slot1", "turn_slot2")):
+            cols = slice(u * half, (u + 1) * half)
+            bank = psum.tile([P, half], F32, name=f"h1_bank{u}", tag=tag)
+            first_product(1, bank[:], cols)
+            nc.scalar.activation(h[1][:, cols], bank[:], RELU)
+        for t in range(2, PACK):
             bank = psum.tile([P, S], F32, name=f"h_bank{t}", tag=f"h_slot{t}")
             first_product(t, bank[:], slice(0, S))
             nc.scalar.activation(h[t][:], bank[:], RELU)

@@ -163,12 +163,12 @@ def tile_picked_zfp_lin_p_kernel(
             bank = psum.tile([P, half], F32, name=f"h1_bank{u}", tag=tag)
             first_product(1, bank[:], cols)
             nc.scalar.activation(h[1][:, cols], bank[:], RELU)
+        e_first = round_e(0, "codes1")
         for t in range(2, PACK):
             bank = psum.tile([P, S], F32, name=f"h_bank{t}", tag=f"h_slot{t}")
             first_product(t, bank[:], slice(0, S))
             nc.scalar.activation(h[t][:], bank[:], RELU)
 
-        e_first = round_e(0, "codes0")
         z_bf = [sbuf(f"z_bf{u}", [P, VH, PACK], BF16) for u in range(2)]
 
         picked = [[sbuf(f"picked{c}_{d}", [P, V], F32, tag=f"picked{c}_{d}") for d in range(2)] for c in range(2)]
@@ -192,16 +192,16 @@ def tile_picked_zfp_lin_p_kernel(
                         scale=gate_cols[d][:, u : u + 1],
                     )
         e_second = round_e(1, "picked1_1")
-        for u in range(2):
-            for t in range(2):
-                for d in range(2):
+        for d in range(2):
+            for u in range(2):
+                for t in range(2):
                     nc.tensor.matmul(
                         z_banks[u][:, t, :],
                         lhsT=gated[u][d][:, t, :],
                         rhs=identity[:],
                         is_transpose=True,
-                        start=(d == 0),
-                        stop=(d == 1),
+                        start=(d == 0 and t == 0),
+                        stop=(d == 1 and t == 1),
                     )
         for u in range(2):
             nc.scalar.copy(z_bf[u][:, :, 0:2], z_banks[u][:].rearrange("p t v -> p v t"))

@@ -124,19 +124,18 @@ def tile_picked_zfp_lin_p_kernel(
             late_bf.rearrange("p t m j -> p (t m j)"),
         )
 
-        def round_e(u, slot):
-            rounded = sbuf(f"e_bf{u}", [P, VH, PACK], BF16, tag=slot)
+        def round_e(cols, slot):
+            rounded = sbuf(f"e_bf{cols.start}", [P, cols.stop - cols.start, PACK], BF16, tag=slot)
             nc.scalar.copy(
                 rounded[:].rearrange("p (c i) j -> p c j i", i=4),
-                e_raw[:, :, u * VH : (u + 1) * VH].rearrange("p j (c i) -> p c j i", i=4),
+                e_raw[:, :, cols].rearrange("p j (c i) -> p c j i", i=4),
             )
             return rounded
 
         e_codes = sbuf("e_codes", [P, V], U32)
         e_scale = sbuf("e_scale", [P, V], U8)
 
-        def quantize_e(u, rounded):
-            cols = slice(u * VH, (u + 1) * VH)
+        def quantize_e(cols, rounded):
             nc.vector.quantize_mx(
                 e_codes[:, cols].bitcast(FP8X4), e_scale[:, cols], rounded[:].rearrange("p v j -> p (v j)")
             )
@@ -163,7 +162,8 @@ def tile_picked_zfp_lin_p_kernel(
             bank = psum.tile([P, half], F32, name=f"h1_bank{u}", tag=tag)
             first_product(1, bank[:], cols)
             nc.scalar.activation(h[1][:, cols], bank[:], RELU)
-        e_first = round_e(0, "codes1")
+        e_parts = [slice(0, V // 4), slice(V // 4, VH), slice(VH, V)]
+        e_first = [round_e(e_parts[c], f"codes{c}") for c in range(2)]
         for t in range(2, PACK):
             bank = psum.tile([P, S], F32, name=f"h_bank{t}", tag=f"h_slot{t}")
             first_product(t, bank[:], slice(0, S))
@@ -175,7 +175,8 @@ def tile_picked_zfp_lin_p_kernel(
         for c in range(2):
             for d in range(2):
                 nc.vector.tensor_copy(picked[c][d][:], h[c][:].indirect(pos_sb[d][:]))
-        quantize_e(0, e_first)
+        for c in range(2):
+            quantize_e(e_parts[c], e_first[c])
 
         z_banks = [psum.tile([P, 2, VH], F32, name=f"z_bank{u}", tag=f"h_slot{u + 1}") for u in range(2)]
         gated = [[sbuf(f"gated{u}_{d}", [P, 2, P], F32) for d in range(2)] for u in range(2)]
@@ -191,7 +192,7 @@ def tile_picked_zfp_lin_p_kernel(
                         COPY,
                         scale=gate_cols[d][:, u : u + 1],
                     )
-        e_second = round_e(1, "picked1_1")
+        e_second = round_e(e_parts[2], "picked1_1")
         for d in range(2):
             for u in range(2):
                 for t in range(2):
@@ -224,7 +225,7 @@ def tile_picked_zfp_lin_p_kernel(
                 terms[1][:, :, cols].rearrange("p t v -> p v t"),
                 ALU.add,
             )
-        quantize_e(1, e_second)
+        quantize_e(e_parts[2], e_second)
         for u in range(2):
             cols = slice(u * VH, (u + 1) * VH)
             z_codes = sbuf(f"z_codes{u}", [P, VH], U32)

@@ -22,6 +22,7 @@ VH = V // 2
 MH = P // 2
 
 X_FIRST = 384
+E_VECTOR = 64
 
 
 def tile_picked_zfp_lin_p_kernel(
@@ -41,6 +42,7 @@ def tile_picked_zfp_lin_p_kernel(
         def load_scales(queue, plane, scales, quadrants=range(4)):
             for q in quadrants:
                 queue.dma_start(plane[32 * q : 32 * q + 4, :].bitcast(I32), scales[0, 4 * q : 4 * q + 4, :].bitcast(I32))
+
 
         offs_sb = sbuf("offs_sb", [P, S // 16], U16)
         pos_sb = [sbuf(f"pos_sb{d}", [P, V // 16], U16) for d in range(2)]
@@ -74,19 +76,19 @@ def tile_picked_zfp_lin_p_kernel(
         nc.sync.dma_start(pos_sb[0][:], pos1)
         nc.sync.dma_start(e_raw[:], eT.rearrange("(p j) v -> p j v", j=PACK))
         nc.sync.dma_start(pos_sb[1][:], pos2)
+        for d in range(2):
+            nc.sync.dma_start(gate_rows[d][:], gate[d])
         with nc.allow_non_contiguous_dma(reason="one gate value a partition"):
             for d in range(2):
                 nc.sync.dma_start(gate_cols[d][:], gate[d, 0, :].rearrange("(u v) -> v u", u=2))
-        for d in range(2):
-            nc.sync.dma_start(gate_rows[d][:], gate[d])
         nc.sync.dma_start(w3w[:], words_of(w3_words))
         nc.sync.dma_start(w2w[:], words_of(w2_words))
         load_scales(nc.sync, w3s, w3_scales)
         load_scales(nc.sync, w2s, w2_scales)
 
-        xs = sbuf("xs", [P, S], U8)
+        xs = sbuf("xs", [P, S], U8, tag="picked_scales")
         nc.vector.tensor_copy(xs[:], xs_all[:].indirect(offs_sb[:]))
-        xw = sbuf("xw", [P, S], U32)
+        xw = sbuf("xw", [P, S], U32, tag="picked_words")
         nc.vector.tensor_copy(xw[:], xw_all[:].bitcast(U32).indirect(offs_sb[:]))
 
         w1_bf = sbuf("w1_bf", [P, 3 * P, PACK], BF16)
@@ -124,21 +126,15 @@ def tile_picked_zfp_lin_p_kernel(
             late_bf.rearrange("p t m j -> p (t m j)"),
         )
 
-        def round_e(cols, slot):
-            rounded = sbuf(f"e_bf{cols.start}", [P, cols.stop - cols.start, PACK], BF16, tag=slot)
-            nc.scalar.copy(
-                rounded[:].rearrange("p (c i) j -> p c j i", i=4),
-                e_raw[:, :, cols].rearrange("p j (c i) -> p c j i", i=4),
-            )
-            return rounded
-
+        e_pool = V - E_VECTOR
+        e_bf = w1_bf[:, :e_pool]
         e_codes = sbuf("e_codes", [P, V], U32)
         e_scale = sbuf("e_scale", [P, V], U8)
+        nc.gpsimd.tensor_scalar(e_bf, e_raw[:, :, :e_pool].rearrange("p j v -> p v j"), 1.0, 0.0, ALU.mult, ALU.add)
 
         def quantize_e(cols, rounded):
-            nc.vector.quantize_mx(
-                e_codes[:, cols].bitcast(FP8X4), e_scale[:, cols], rounded[:].rearrange("p v j -> p (v j)")
-            )
+            nc.vector.quantize_mx(e_codes[:, cols].bitcast(FP8X4), e_scale[:, cols], rounded.rearrange("p v j -> p (v j)"))
+
 
         def first_product(t, bank, cols):
             nc.tensor.matmul_mx(
@@ -161,40 +157,59 @@ def tile_picked_zfp_lin_p_kernel(
             cols = slice(u * half, (u + 1) * half)
             bank = psum.tile([P, half], F32, name=f"h1_bank{u}", tag=tag)
             first_product(1, bank[:], cols)
-            nc.scalar.activation(h[1][:, cols], bank[:], RELU)
-        e_parts = [slice(0, V // 4), slice(V // 4, VH), slice(VH, V)]
-        e_first = [round_e(e_parts[c], f"codes{c}") for c in range(2)]
-        for t in range(2, PACK):
-            bank = psum.tile([P, S], F32, name=f"h_bank{t}", tag=f"h_slot{t}")
-            first_product(t, bank[:], slice(0, S))
-            nc.scalar.activation(h[t][:], bank[:], RELU)
+            nc.vector.tensor_scalar(h[1][:, cols], bank[:], 0.0, None, ALU.max)
+        for u in range(2):
+            cols = slice(u * half, (u + 1) * half)
+            bank = psum.tile([P, half], F32, name=f"h2_bank{u}", tag=f"half_bank{u}")
+            first_product(2, bank[:], cols)
+            nc.vector.tensor_scalar(h[2][:, cols], bank[:], 0.0, None, ALU.max)
+        h3_bank = psum.tile([P, S], F32, name="h3_bank", tag="h_slot3")
+        first_product(3, h3_bank[:], slice(0, S))
+        e_tail = sbuf("e_tail", [P, E_VECTOR, PACK], BF16, tag="picked_scales")
+        nc.vector.tensor_copy(
+            e_tail[:].rearrange("p (c i) j -> p c j i", i=4), e_raw[:, :, e_pool:].rearrange("p j (c i) -> p c j i", i=4)
+        )
+        quantize_e(slice(0, VH), e_bf[:, :VH])
+        quantize_e(slice(VH, e_pool), e_bf[:, VH:])
+        quantize_e(slice(e_pool, V), e_tail[:])
+        whole = (slice(0, V), slice(0, V // 16))
+        halves = [(slice(u * VH, (u + 1) * VH), slice(u * VH // 16, (u + 1) * VH // 16)) for u in range(2)]
+        picked = {}
+
+        def gather_plain(c, d, parts, tag=""):
+            lists = slice(halves[parts[0]][1].start, halves[parts[-1]][1].stop)
+            tile = sbuf(f"picked{c}_{d}_{parts[0]}", [P, len(parts), VH], F32, tag=tag)
+            nc.scalar.activation(tile[:].rearrange("p u v -> p (u v)"), h[c][:].indirect(pos_sb[d][:, lists]), COPY)
+            for n, u in enumerate(parts):
+                picked[c, d, u] = tile[:, n]
+
+        gather_plain(0, 0, (0, 1))
+        gather_plain(0, 1, (0, 1))
+        gather_plain(1, 0, (0, 1))
+        gather_plain(1, 1, (0,))
+        nc.scalar.activation(h[3][:], h3_bank[:], RELU)
+        gather_plain(1, 1, (1,), tag="picked_words")
 
         z_bf = [sbuf(f"z_bf{u}", [P, VH, PACK], BF16) for u in range(2)]
-
-        picked = [[sbuf(f"picked{c}_{d}", [P, V], F32, tag=f"picked{c}_{d}") for d in range(2)] for c in range(2)]
-        for c in range(2):
-            for d in range(2):
-                nc.vector.tensor_copy(picked[c][d][:], h[c][:].indirect(pos_sb[d][:]))
-        for c in range(2):
-            quantize_e(e_parts[c], e_first[c])
-
         z_banks = [psum.tile([P, 2, VH], F32, name=f"z_bank{u}", tag=f"h_slot{u + 1}") for u in range(2)]
         gated = [[sbuf(f"gated{u}_{d}", [P, 2, P], F32) for d in range(2)] for u in range(2)]
+        first_turned = psum.tile([P, 2, 2, P], F32, name="first_turned", tag="turn_slot0")
+        turned = [
+            [first_turned[:, u] for u in range(2)],
+            [psum.tile([P, 2, P], F32, name=f"second_turned{u}", tag=f"turn_slot{u + 1}")[:] for u in range(2)],
+        ]
         for c in range(2):
             for d in range(2):
-                turned = psum.tile([P, 2, P], F32, name=f"turned{c}_{d}", tag=f"turn_slot{(2 * c + d) % 3}")
                 for u in range(2):
-                    nc.tensor.transpose(turned[:, u, :], picked[c][d][:, u * VH : (u + 1) * VH], identity[:])
-                for u in range(2):
-                    nc.scalar.activation(
-                        gated[u][d][:, :, c * MH : (c + 1) * MH],
-                        turned[:, u, :].rearrange("p (t m) -> p t m", t=2),
-                        COPY,
-                        scale=gate_cols[d][:, u : u + 1],
-                    )
-        e_second = round_e(e_parts[2], "picked1_1")
-        for d in range(2):
-            for u in range(2):
+                    nc.tensor.transpose(turned[d][u][:, c, :], picked[c, d, u], identity[:])
+        for u in range(2):
+            for d in range(2):
+                nc.scalar.activation(
+                    gated[u][d][:].rearrange("p t (c m) -> p c t m", c=2),
+                    turned[d][u].rearrange("p c (t m) -> p c t m", t=2),
+                    COPY,
+                    scale=gate_cols[d][:, u : u + 1],
+                )
                 for t in range(2):
                     nc.tensor.matmul(
                         z_banks[u][:, t, :],
@@ -207,12 +222,10 @@ def tile_picked_zfp_lin_p_kernel(
         for u in range(2):
             nc.scalar.copy(z_bf[u][:, :, 0:2], z_banks[u][:].rearrange("p t v -> p v t"))
 
-        whole = [(slice(0, V), slice(0, V // 16))]
-        halves = [(slice(u * VH, (u + 1) * VH), slice(u * VH // 16, (u + 1) * VH // 16)) for u in range(2)]
         terms = [sbuf(f"terms{d}", [P, 2, V], F32) for d in range(2)]
         for t in range(2):
             for d in range(2):
-                for cols, lists in halves if (t, d) == (1, 1) else whole:
+                for cols, lists in halves if (t, d) == (1, 1) else [whole]:
                     nc.vector.tensor_tensor(
                         terms[d][:, t, cols], h[2 + t][:].indirect(pos_sb[d][:, lists]), gate_rows[d][:, cols], ALU.mult
                     )
@@ -225,7 +238,6 @@ def tile_picked_zfp_lin_p_kernel(
                 terms[1][:, :, cols].rearrange("p t v -> p v t"),
                 ALU.add,
             )
-        quantize_e(e_parts[2], e_second)
         for u in range(2):
             cols = slice(u * VH, (u + 1) * VH)
             z_codes = sbuf(f"z_codes{u}", [P, VH], U32)

@@ -204,12 +204,13 @@ def tile_picked_zfp_lin_p_kernel(
                     nc.tensor.transpose(turned[d][u][:, c, :], picked[c, d, u], identity[:])
         for u in range(2):
             for d in range(2):
-                nc.scalar.activation(
-                    gated[u][d][:].rearrange("p t (c m) -> p c t m", c=2),
-                    turned[d][u].rearrange("p c (t m) -> p c t m", t=2),
-                    COPY,
-                    scale=gate_cols[d][:, u : u + 1],
-                )
+                for slots in (slice(0, 1), slice(1, 2)) if (u, d) == (1, 1) else (slice(0, 2),):
+                    nc.scalar.activation(
+                        gated[u][d][:].rearrange("p t (c m) -> p c t m", c=2)[:, :, slots],
+                        turned[d][u].rearrange("p c (t m) -> p c t m", t=2)[:, :, slots],
+                        COPY,
+                        scale=gate_cols[d][:, u : u + 1],
+                    )
                 for t in range(2):
                     nc.tensor.matmul(
                         z_banks[u][:, t, :],
@@ -243,7 +244,7 @@ def tile_picked_zfp_lin_p_kernel(
             z_codes = sbuf(f"z_codes{u}", [P, VH], U32)
             z_scale = sbuf(f"z_scale{u}", [P, VH], U8)
             nc.vector.quantize_mx(z_codes[:].bitcast(FP8X4), z_scale[:], z_bf[u][:].rearrange("p v t -> p (v t)"))
-            bank = psum.tile([P, VH], F32, name=f"out_bank{u}", tag=f"half_bank{u}")
+            bank = psum.tile([P, VH], F32, name=f"out_bank{u}", tag=("half_bank0", "turn_slot2")[u])
             nc.tensor.matmul_mx(
                 bank[:],
                 lhsT=w3w[:].bitcast(FP8X4),

@@ -21,7 +21,6 @@ COPY = mybir.ActivationFunctionType.Copy
 VH = V // 2
 MH = P // 2
 
-X_FIRST = 384
 E_VECTOR = 64
 
 
@@ -49,7 +48,7 @@ def tile_picked_zfp_lin_p_kernel(
         xw_all = sbuf("xw_all", [P, T], I32)
         xs_all = sbuf("xs_all", [P, T], U8)
         w1_raw = [sbuf(f"w1_raw{c}", [P, PACK, H // 2], F32) for c in range(2)]
-        gate_rows = [sbuf(f"gate_rows{d}", [P, V], F32) for d in range(2)]
+        gate_rows = sbuf("gate_rows", [P, 2, V], F32)
         gate_cols = [sbuf(f"gate_cols{d}", [P, 2], F32) for d in range(2)]
         identity = sbuf("identity", [P, P], F32)
         e_raw = sbuf("e_raw", [P, PACK, V], F32)
@@ -64,20 +63,23 @@ def tile_picked_zfp_lin_p_kernel(
         make_identity(nc, identity[:])
 
         nc.sync.dma_start(offs_sb[:], offs)
-        nc.sync.dma_start(xw_all[:, :X_FIRST], words_of(x_words)[:, :X_FIRST])
-        load_scales(nc.scalar, xs_all, x_scales, range(2))
-        load_scales(nc.sync, xs_all, x_scales, range(2, 4))
-        nc.sync.dma_start(xw_all[:, X_FIRST:], words_of(x_words)[:, X_FIRST:])
         w1_rows = w1.rearrange("(p j) c -> p j c", j=PACK)
         pairs = [slice(0, 2), slice(2, 4)]
-        for c in range(2):
-            for pair in pairs:
-                nc.sync.dma_start(w1_raw[c][:, pair], w1_rows[:, pair, c * H // 2 : (c + 1) * H // 2])
+
+        def load_w1(c, pair):
+            nc.sync.dma_start(w1_raw[c][:, pair], w1_rows[:, pair, c * H // 2 : (c + 1) * H // 2])
+
+        load_w1(0, pairs[0])
+        load_scales(nc.scalar, xs_all, x_scales, range(2))
+        load_scales(nc.sync, xs_all, x_scales, range(2, 4))
+        nc.sync.dma_start(xw_all[:], words_of(x_words))
+        load_w1(0, pairs[1])
+        for pair in pairs:
+            load_w1(1, pair)
         nc.sync.dma_start(pos_sb[0][:], pos1)
-        nc.sync.dma_start(e_raw[:], eT.rearrange("(p j) v -> p j v", j=PACK))
         nc.sync.dma_start(pos_sb[1][:], pos2)
-        for d in range(2):
-            nc.sync.dma_start(gate_rows[d][:], gate[d])
+        nc.sync.dma_start(e_raw[:], eT.rearrange("(p j) v -> p j v", j=PACK))
+        nc.sync.dma_start(gate_rows[:], gate.rearrange("d p v -> p d v"))
         with nc.allow_non_contiguous_dma(reason="one gate value a partition"):
             for d in range(2):
                 nc.sync.dma_start(gate_cols[d][:], gate[d, 0, :].rearrange("(u v) -> v u", u=2))
@@ -102,29 +104,24 @@ def tile_picked_zfp_lin_p_kernel(
                 w1_raw[c][:].rearrange("p j (m g t) -> p g m t j", g=2, t=2)[:, g, rows, :, slots],
             )
 
-        late_codes = sbuf("late_codes", [P, 2, P], U32)
-        w1_codes = [sbuf(f"w1_codes{t}", [P, P], U32, tag=f"codes{t}")[:] for t in range(2)] + [late_codes[:, t] for t in range(2)]
-        late_scale = sbuf("late_scale", [P, 2, P], U8)
-        w1_scale = [sbuf(f"w1_scale{t}", [P, P], U8)[:] for t in range(2)] + [late_scale[:, t] for t in range(2)]
+        w1_codes = [sbuf(f"w1_codes{t}", [P, P], U32, tag=f"codes{t}")[:] for t in range(PACK)]
+        w1_scale = [sbuf(f"w1_scale{t}", [P, P], U8)[:] for t in range(PACK)]
 
         def quantize_early(c, rounded):
             nc.vector.quantize_mx(w1_codes[c].bitcast(FP8X4), w1_scale[c], rounded.rearrange("p t m j -> p (t m j)"))
 
         half = S // 2
-        for pair in range(2):
-            round_w1(nc.scalar.copy, first_bf, 0, 0, slice(0, MH), slice(2 * pair, 2 * pair + 2))
+        for pair in pairs:
+            round_w1(nc.scalar.copy, first_bf, 0, 0, slice(0, MH), pair)
+            round_w1(nc.scalar.copy, late_bf[:, :, :MH], 0, 1, slice(0, MH), pair)
         quantize_early(0, first_bf)
-        round_w1(nc.scalar.copy, late_bf[:, :, :MH], 0, 1, slice(0, MH))
         round_w1(nc.scalar.copy, late_bf[:, :, MH:], 1, 1, slice(0, MH), pairs[0])
         for pair in pairs:
             round_w1(nc.vector.tensor_copy, second_bf, 1, 0, slice(0, MH), pair)
         round_w1(nc.vector.tensor_copy, late_bf[:, :, MH:], 1, 1, slice(0, MH), pairs[1])
         quantize_early(1, second_bf)
-        nc.vector.quantize_mx(
-            late_codes[:].rearrange("p t m -> p (t m)").bitcast(FP8X4),
-            late_scale[:].rearrange("p t m -> p (t m)"),
-            late_bf.rearrange("p t m j -> p (t m j)"),
-        )
+        for t in range(2):
+            quantize_early(2 + t, late_bf[:, t : t + 1])
 
         e_pool = V - E_VECTOR
         e_bf = w1_bf[:, :e_pool]
@@ -153,7 +150,7 @@ def tile_picked_zfp_lin_p_kernel(
             first_product(0, h0_banks[u][:], slice(u * half, (u + 1) * half))
         for u in range(2):
             nc.scalar.activation(h[0][:, u * half : (u + 1) * half], h0_banks[u][:], RELU)
-        for u, tag in enumerate(("h_slot1", "turn_slot2")):
+        for u, tag in enumerate(("tile1_bank0", "tile1_bank1")):
             cols = slice(u * half, (u + 1) * half)
             bank = psum.tile([P, half], F32, name=f"h1_bank{u}", tag=tag)
             first_product(1, bank[:], cols)
@@ -163,9 +160,9 @@ def tile_picked_zfp_lin_p_kernel(
             bank = psum.tile([P, half], F32, name=f"h2_bank{u}", tag=f"half_bank{u}")
             first_product(2, bank[:], cols)
             nc.vector.tensor_scalar(h[2][:, cols], bank[:], 0.0, None, ALU.max)
-        h3_bank = psum.tile([P, S], F32, name="h3_bank", tag="h_slot3")
+        h3_bank = psum.tile([P, S], F32, name="h3_bank", tag="tile1_bank0")
         first_product(3, h3_bank[:], slice(0, S))
-        e_tail = sbuf("e_tail", [P, E_VECTOR, PACK], BF16, tag="picked_scales")
+        e_tail = sbuf("e_tail", [P, E_VECTOR, PACK], BF16, tag="codes2")
         nc.vector.tensor_copy(
             e_tail[:].rearrange("p (c i) j -> p c j i", i=4), e_raw[:, :, e_pool:].rearrange("p j (c i) -> p c j i", i=4)
         )
@@ -191,12 +188,12 @@ def tile_picked_zfp_lin_p_kernel(
         gather_plain(1, 1, (1,), tag="picked_words")
 
         z_bf = [sbuf(f"z_bf{u}", [P, VH, PACK], BF16) for u in range(2)]
-        z_banks = [psum.tile([P, 2, VH], F32, name=f"z_bank{u}", tag=f"h_slot{u + 1}") for u in range(2)]
+        z_banks = [psum.tile([P, 2, VH], F32, name=f"z_bank{u}") for u in range(2)]
         gated = [[sbuf(f"gated{u}_{d}", [P, 2, P], F32) for d in range(2)] for u in range(2)]
-        first_turned = psum.tile([P, 2, 2, P], F32, name="first_turned", tag="turn_slot0")
+        first_turned = psum.tile([P, 2, 2, P], F32, name="first_turned", tag="tile1_bank1")
         turned = [
             [first_turned[:, u] for u in range(2)],
-            [psum.tile([P, 2, P], F32, name=f"second_turned{u}", tag=f"turn_slot{u + 1}")[:] for u in range(2)],
+            [psum.tile([P, 2, P], F32, name=f"second_turned{u}", tag=f"half_bank{u}")[:] for u in range(2)],
         ]
         for c in range(2):
             for d in range(2):
@@ -228,7 +225,7 @@ def tile_picked_zfp_lin_p_kernel(
             for d in range(2):
                 for cols, lists in halves if (t, d) == (1, 1) else [whole]:
                     nc.vector.tensor_tensor(
-                        terms[d][:, t, cols], h[2 + t][:].indirect(pos_sb[d][:, lists]), gate_rows[d][:, cols], ALU.mult
+                        terms[d][:, t, cols], h[2 + t][:].indirect(pos_sb[d][:, lists]), gate_rows[:, d, cols], ALU.mult
                     )
 
         for u in range(2):
@@ -244,7 +241,7 @@ def tile_picked_zfp_lin_p_kernel(
             z_codes = sbuf(f"z_codes{u}", [P, VH], U32)
             z_scale = sbuf(f"z_scale{u}", [P, VH], U8)
             nc.vector.quantize_mx(z_codes[:].bitcast(FP8X4), z_scale[:], z_bf[u][:].rearrange("p v t -> p (v t)"))
-            bank = psum.tile([P, VH], F32, name=f"out_bank{u}", tag=("half_bank0", "turn_slot2")[u])
+            bank = psum.tile([P, VH], F32, name=f"out_bank{u}", tag=("out_bank0", "half_bank1")[u])
             nc.tensor.matmul_mx(
                 bank[:],
                 lhsT=w3w[:].bitcast(FP8X4),

@@ -21,6 +21,7 @@ COPY = mybir.ActivationFunctionType.Copy
 VH = V // 2
 MH = P // 2
 
+X_FIRST = 384
 E_VECTOR = 64
 
 
@@ -63,19 +64,15 @@ def tile_picked_zfp_lin_p_kernel(
         make_identity(nc, identity[:])
 
         nc.sync.dma_start(offs_sb[:], offs)
-        w1_rows = w1.rearrange("(p j) c -> p j c", j=PACK)
-        pairs = [slice(0, 2), slice(2, 4)]
-
-        def load_w1(c, pair):
-            nc.sync.dma_start(w1_raw[c][:, pair], w1_rows[:, pair, c * H // 2 : (c + 1) * H // 2])
-
-        load_w1(0, pairs[0])
+        nc.sync.dma_start(xw_all[:, :X_FIRST], words_of(x_words)[:, :X_FIRST])
         load_scales(nc.scalar, xs_all, x_scales, range(2))
         load_scales(nc.sync, xs_all, x_scales, range(2, 4))
-        nc.sync.dma_start(xw_all[:], words_of(x_words))
-        load_w1(0, pairs[1])
-        for pair in pairs:
-            load_w1(1, pair)
+        nc.sync.dma_start(xw_all[:, X_FIRST:], words_of(x_words)[:, X_FIRST:])
+        w1_rows = w1.rearrange("(p j) c -> p j c", j=PACK)
+        pairs = [slice(0, 2), slice(2, 4)]
+        for c in range(2):
+            for pair in pairs:
+                nc.sync.dma_start(w1_raw[c][:, pair], w1_rows[:, pair, c * H // 2 : (c + 1) * H // 2])
         nc.sync.dma_start(pos_sb[0][:], pos1)
         nc.sync.dma_start(pos_sb[1][:], pos2)
         nc.sync.dma_start(e_raw[:], eT.rearrange("(p j) v -> p j v", j=PACK))
@@ -113,8 +110,8 @@ def tile_picked_zfp_lin_p_kernel(
         half = S // 2
         for pair in pairs:
             round_w1(nc.scalar.copy, first_bf, 0, 0, slice(0, MH), pair)
-            round_w1(nc.scalar.copy, late_bf[:, :, :MH], 0, 1, slice(0, MH), pair)
         quantize_early(0, first_bf)
+        round_w1(nc.scalar.copy, late_bf[:, :, :MH], 0, 1, slice(0, MH))
         round_w1(nc.scalar.copy, late_bf[:, :, MH:], 1, 1, slice(0, MH), pairs[0])
         for pair in pairs:
             round_w1(nc.vector.tensor_copy, second_bf, 1, 0, slice(0, MH), pair)

@@ -50,7 +50,7 @@ def tile_picked_zfp_lin_p_kernel(
         xs_all = sbuf("xs_all", [P, T], U8)
         w1_raw = [sbuf(f"w1_raw{c}", [P, PACK, H // 2], F32) for c in range(2)]
         gate_rows = sbuf("gate_rows", [P, 2, V], F32)
-        gate_cols = [sbuf(f"gate_cols{d}", [P, 2], F32) for d in range(2)]
+        gate_cols = sbuf("gate_cols", [P, 4], F32)
         identity = sbuf("identity", [P, P], F32)
         e_raw = sbuf("e_raw", [P, PACK, V], F32)
         w2w = sbuf("w2w", [P, N], I32)
@@ -74,12 +74,12 @@ def tile_picked_zfp_lin_p_kernel(
             for pair in pairs:
                 nc.sync.dma_start(w1_raw[c][:, pair], w1_rows[:, pair, c * H // 2 : (c + 1) * H // 2])
         nc.sync.dma_start(pos_sb[0][:], pos1)
-        nc.sync.dma_start(pos_sb[1][:], pos2)
         nc.sync.dma_start(e_raw[:], eT.rearrange("(p j) v -> p j v", j=PACK))
+        nc.sync.dma_start(pos_sb[1][:], pos2)
         nc.sync.dma_start(gate_rows[:], gate.rearrange("d p v -> p d v"))
         with nc.allow_non_contiguous_dma(reason="one gate value a partition"):
-            for d in range(2):
-                nc.sync.dma_start(gate_cols[d][:], gate[d, 0, :].rearrange("(u v) -> v u", u=2))
+            half_rows = gate.rearrange("d p (u v) -> (d p u) v", u=2)
+            nc.sync.dma_start(gate_cols[:], half_rows[0 : 3 * (P + 1) + 1 : P + 1].rearrange("k v -> v k"))
         nc.sync.dma_start(w3w[:], words_of(w3_words))
         nc.sync.dma_start(w2w[:], words_of(w2_words))
         load_scales(nc.sync, w3s, w3_scales)
@@ -203,7 +203,7 @@ def tile_picked_zfp_lin_p_kernel(
                         gated[u][d][:].rearrange("p t (c m) -> p c t m", c=2)[:, :, slots],
                         turned[d][u].rearrange("p c (t m) -> p c t m", t=2)[:, :, slots],
                         COPY,
-                        scale=gate_cols[d][:, u : u + 1],
+                        scale=gate_cols[:, 2 * d + u : 2 * d + u + 1],
                     )
                 for t in range(2):
                     nc.tensor.matmul(

from contextlib import ExitStack

import concourse.mybir as mybir
from concourse.masks import make_identity

K, T, S, V, H, N = 512, 1024, 512, 256, 512, 128
P = 128
PACK = 4
FLOPS = 2 * K * H * S + 2 * H * N * V + 2 * K * N * V

F32 = mybir.dt.float32
BF16 = mybir.dt.bfloat16
I32 = mybir.dt.int32
U32 = mybir.dt.uint32
U16 = mybir.dt.uint16
U8 = mybir.dt.uint8
FP8X4 = mybir.dt.float8_e4m3fn_x4
ALU = mybir.AluOpType
RELU = mybir.ActivationFunctionType.Relu
COPY = mybir.ActivationFunctionType.Copy
VH = V // 2
MH = P // 2

X_FIRST = 384
E_VECTOR = 64


def tile_picked_zfp_lin_p_kernel(
    tc, x_words, x_scales, w1, w2_words, w2_scales, gate, eT, w3_words, w3_scales, offs, pos1, pos2, out
):
    nc = tc.nc
    with ExitStack() as ctx:
        keep = ctx.enter_context(tc.tile_pool(name="keep", bufs=1))
        psum = ctx.enter_context(tc.psum_pool(name="psum", bufs=1))

        def sbuf(name, shape, dtype, tag=""):
            return keep.tile(shape, dtype, name=name, align_bytes=64, tag=tag)

        def words_of(packed):
            return packed[0].rearrange("p c r -> p (c r)").bitcast(I32)

        def load_scales(queue, plane, scales, quadrants=range(4)):
            for q in quadrants:
                queue.dma_start(plane[32 * q : 32 * q + 4, :].bitcast(I32), scales[0, 4 * q : 4 * q + 4, :].bitcast(I32))


        offs_sb = sbuf("offs_sb", [P, S // 16], U16)
        pos_sb = [sbuf(f"pos_sb{d}", [P, V // 16], U16) for d in range(2)]
        xw_all = sbuf("xw_all", [P, T], I32)
        xs_all = sbuf("xs_all", [P, T], U8)
        w1_raw = [sbuf(f"w1_raw{c}", [P, PACK, H // 2], F32) for c in range(2)]
        gate_rows = sbuf("gate_rows", [P, 2, V], F32)
        gate_cols = sbuf("gate_cols", [P, 4], F32)
        identity = sbuf("identity", [P, P], F32)
        e_raw = sbuf("e_raw", [P, PACK, V], F32)
        w2w = sbuf("w2w", [P, N], I32)
        w3w = sbuf("w3w", [P, N], I32)
        w2s = sbuf("w2s", [P, N], U8)
        w3s = sbuf("w3s", [P, N], U8)

        nc.gpsimd.memset(xs_all[:].bitcast(I32), 0)
        nc.gpsimd.memset(w3s[:].bitcast(I32), 0)
        nc.gpsimd.memset(w2s[:].bitcast(I32), 0)
        make_identity(nc, identity[:])

        nc.sync.dma_start(offs_sb[:], offs)
        nc.sync.dma_start(xw_all[:, :X_FIRST], words_of(x_words)[:, :X_FIRST])
        load_scales(nc.scalar, xs_all, x_scales, range(2))
        load_scales(nc.sync, xs_all, x_scales, range(2, 4))
        nc.sync.dma_start(xw_all[:, X_FIRST:], words_of(x_words)[:, X_FIRST:])
        w1_rows = w1.rearrange("(p j) c -> p j c", j=PACK)
        pairs = [slice(0, 2), slice(2, 4)]
        for c in range(2):
            for pair in pairs:
                nc.sync.dma_start(w1_raw[c][:, pair], w1_rows[:, pair, c * H // 2 : (c + 1) * H // 2])
        nc.sync.dma_start(pos_sb[0][:], pos1)
        nc.sync.dma_start(e_raw[:], eT.rearrange("(p j) v -> p j v", j=PACK))
        nc.sync.dma_start(pos_sb[1][:], pos2)
        nc.sync.dma_start(gate_rows[:], gate.rearrange("d p v -> p d v"))
        with nc.allow_non_contiguous_dma(reason="one gate value a partition"):
            half_rows = gate.rearrange("d p (u v) -> (d p u) v", u=2)
            nc.sync.dma_start(gate_cols[:], half_rows[0 : 3 * (P + 1) + 1 : P + 1].rearrange("k v -> v k"))
        nc.sync.dma_start(w3w[:], words_of(w3_words))
        nc.sync.dma_start(w2w[:], words_of(w2_words))
        load_scales(nc.sync, w3s, w3_scales)
        load_scales(nc.sync, w2s, w2_scales)

        xs = sbuf("xs", [P, S], U8, tag="picked_scales")
        nc.vector.tensor_copy(xs[:], xs_all[:].indirect(offs_sb[:]))
        xw = sbuf("xw", [P, S], U32, tag="picked_words")
        nc.vector.tensor_copy(xw[:], xw_all[:].bitcast(U32).indirect(offs_sb[:]))

        w1_bf = sbuf("w1_bf", [P, 3 * P, PACK], BF16)
        late_bf = w1_bf[:, : 2 * P].rearrange("p (t m) j -> p t m j", t=2)
        second_bf = w1_bf[:, 2 * P :].rearrange("p (t m) j -> p t m j", t=2)
        first_bf = w1_bf[:, 2 * P - MH : 3 * P - MH].rearrange("p (t m) j -> p t m j", t=2)

        def round_w1(engine_copy, target, c, g, rows, slots=slice(0, PACK)):
            engine_copy(
                target.rearrange("p t m j -> p m t j")[:, rows, :, slots],
                w1_raw[c][:].rearrange("p j (m g t) -> p g m t j", g=2, t=2)[:, g, rows, :, slots],
            )

        w1_codes = [sbuf(f"w1_codes{t}", [P, P], U32, tag=f"codes{t}")[:] for t in range(PACK)]
        w1_scale = [sbuf(f"w1_scale{t}", [P, P], U8)[:] for t in range(PACK)]

        def quantize_early(c, rounded):
            nc.vector.quantize_mx(w1_codes[c].bitcast(FP8X4), w1_scale[c], rounded.rearrange("p t m j -> p (t m j)"))

        half = S // 2
        for pair in pairs:
            round_w1(nc.scalar.copy, first_bf, 0, 0, slice(0, MH), pair)
        quantize_early(0, first_bf)
        round_w1(nc.scalar.copy, late_bf[:, :, :MH], 0, 1, slice(0, MH))
        round_w1(nc.scalar.copy, late_bf[:, :, MH:], 1, 1, slice(0, MH), pairs[0])
        for pair in pairs:
            round_w1(nc.vector.tensor_copy, second_bf, 1, 0, slice(0, MH), pair)
        round_w1(nc.vector.tensor_copy, late_bf[:, :, MH:], 1, 1, slice(0, MH), pairs[1])
        quantize_early(1, second_bf)
        for t in range(2):
            quantize_early(2 + t, late_bf[:, t : t + 1])

        e_pool = V - E_VECTOR
        e_bf = w1_bf[:, :e_pool]
        e_codes = sbuf("e_codes", [P, V], U32)
        e_scale = sbuf("e_scale", [P, V], U8)
        nc.gpsimd.tensor_scalar(e_bf, e_raw[:, :, :e_pool].rearrange("p j v -> p v j"), 1.0, 0.0, ALU.mult, ALU.add)

        def quantize_e(cols, rounded):
            nc.vector.quantize_mx(e_codes[:, cols].bitcast(FP8X4), e_scale[:, cols], rounded.rearrange("p v j -> p (v j)"))


        def first_product(t, bank, cols):
            nc.tensor.matmul_mx(
                bank,
                lhsT=w1_codes[t].bitcast(FP8X4),
                lhsT_scale=w1_scale[t],
                rhs=xw[:, cols].bitcast(FP8X4),
                rhs_scale=xs[:, cols],
                start=True,
                stop=True,
            )

        h = [sbuf(f"h{t}", [P, S], F32) for t in range(PACK)]
        h0_banks = [psum.tile([P, half], F32, name=f"h0_bank{u}", tag=f"half_bank{u}") for u in range(2)]
        for u in range(2):
            first_product(0, h0_banks[u][:], slice(u * half, (u + 1) * half))
        for u in range(2):
            nc.scalar.activation(h[0][:, u * half : (u + 1) * half], h0_banks[u][:], RELU)
        for u, tag in enumerate(("tile1_bank0", "tile1_bank1")):
            cols = slice(u * half, (u + 1) * half)
            bank = psum.tile([P, half], F32, name=f"h1_bank{u}", tag=tag)
            first_product(1, bank[:], cols)
            nc.vector.tensor_scalar(h[1][:, cols], bank[:], 0.0, None, ALU.max)
        for u in range(2):
            cols = slice(u * half, (u + 1) * half)
            bank = psum.tile([P, half], F32, name=f"h2_bank{u}", tag=f"half_bank{u}")
            first_product(2, bank[:], cols)
            nc.vector.tensor_scalar(h[2][:, cols], bank[:], 0.0, None, ALU.max)
        h3_bank = psum.tile([P, S], F32, name="h3_bank", tag="tile1_bank0")
        first_product(3, h3_bank[:], slice(0, S))
        e_tail = sbuf("e_tail", [P, E_VECTOR, PACK], BF16, tag="codes2")
        nc.vector.tensor_copy(
            e_tail[:].rearrange("p (c i) j -> p c j i", i=4), e_raw[:, :, e_pool:].rearrange("p j (c i) -> p c j i", i=4)
        )
        quantize_e(slice(0, VH), e_bf[:, :VH])
        quantize_e(slice(VH, e_pool), e_bf[:, VH:])
        quantize_e(slice(e_pool, V), e_tail[:])
        whole = (slice(0, V), slice(0, V // 16))
        halves = [(slice(u * VH, (u + 1) * VH), slice(u * VH // 16, (u + 1) * VH // 16)) for u in range(2)]
        picked = {}

        def gather_plain(c, d, parts, tag=""):
            lists = slice(halves[parts[0]][1].start, halves[parts[-1]][1].stop)
            tile = sbuf(f"picked{c}_{d}_{parts[0]}", [P, len(parts), VH], F32, tag=tag)
            nc.scalar.activation(tile[:].rearrange("p u v -> p (u v)"), h[c][:].indirect(pos_sb[d][:, lists]), COPY)
            for n, u in enumerate(parts):
                picked[c, d, u] = tile[:, n]

        gather_plain(0, 0, (0, 1))
        gather_plain(0, 1, (0, 1))
        gather_plain(1, 0, (0, 1))
        gather_plain(1, 1, (0,))
        nc.scalar.activation(h[3][:], h3_bank[:], RELU)
        gather_plain(1, 1, (1,), tag="picked_words")

        z_bf = [sbuf(f"z_bf{u}", [P, VH, PACK], BF16) for u in range(2)]
        z_banks = [psum.tile([P, 2, VH], F32, name=f"z_bank{u}") for u in range(2)]
        gated = [[sbuf(f"gated{u}_{d}", [P, 2, P], F32) for d in range(2)] for u in range(2)]
        first_turned = psum.tile([P, 2, 2, P], F32, name="first_turned", tag="tile1_bank1")
        turned = [
            [first_turned[:, u] for u in range(2)],
            [psum.tile([P, 2, P], F32, name=f"second_turned{u}", tag=f"half_bank{u}")[:] for u in range(2)],
        ]
        for c in range(2):
            for d in range(2):
                for u in range(2):
                    nc.tensor.transpose(turned[d][u][:, c, :], picked[c, d, u], identity[:])
        for u in range(2):
            for d in range(2):
                for slots in (slice(0, 1), slice(1, 2)) if (u, d) == (1, 1) else (slice(0, 2),):
                    nc.scalar.activation(
                        gated[u][d][:].rearrange("p t (c m) -> p c t m", c=2)[:, :, slots],
                        turned[d][u].rearrange("p c (t m) -> p c t m", t=2)[:, :, slots],
                        COPY,
                        scale=gate_cols[:, 2 * d + u : 2 * d + u + 1],
                    )
                for t in range(2):
                    nc.tensor.matmul(
                        z_banks[u][:, t, :],
                        lhsT=gated[u][d][:, t, :],
                        rhs=identity[:],
                        is_transpose=True,
                        start=(d == 0 and t == 0),
                        stop=(d == 1 and t == 1),
                    )
        for u in range(2):
            nc.scalar.copy(z_bf[u][:, :, 0:2], z_banks[u][:].rearrange("p t v -> p v t"))

        terms = [sbuf(f"terms{d}", [P, 2, V], F32) for d in range(2)]
        for t in range(2):
            for d in range(2):
                for cols, lists in halves if (t, d) == (1, 1) else [whole]:
                    nc.vector.tensor_tensor(
                        terms[d][:, t, cols], h[2 + t][:].indirect(pos_sb[d][:, lists]), gate_rows[:, d, cols], ALU.mult
                    )

        for u in range(2):
            cols = slice(u * VH, (u + 1) * VH)
            nc.vector.tensor_tensor(
                z_bf[u][:, :, 2:4],
                terms[0][:, :, cols].rearrange("p t v -> p v t"),
                terms[1][:, :, cols].rearrange("p t v -> p v t"),
                ALU.add,
            )
        for u in range(2):
            cols = slice(u * VH, (u + 1) * VH)
            z_codes = sbuf(f"z_codes{u}", [P, VH], U32)
            z_scale = sbuf(f"z_scale{u}", [P, VH], U8)
            nc.vector.quantize_mx(z_codes[:].bitcast(FP8X4), z_scale[:], z_bf[u][:].rearrange("p v t -> p (v t)"))
            bank = psum.tile([P, VH], F32, name=f"out_bank{u}", tag=("out_bank0", "half_bank1")[u])
            nc.tensor.matmul_mx(
                bank[:],
                lhsT=w3w[:].bitcast(FP8X4),
                lhsT_scale=w3s[:],
                rhs=e_codes[:, cols].bitcast(FP8X4),
                rhs_scale=e_scale[:, cols],
                start=True,
                stop=False,
            )
            nc.tensor.matmul_mx(
                bank[:],
                lhsT=w2w[:].bitcast(FP8X4),
                lhsT_scale=w2s[:],
                rhs=z_codes[:].bitcast(FP8X4),
                rhs_scale=z_scale[:],
                start=False,
                stop=True,
            )
            result = sbuf(f"result{u}", [P, VH], F32)
            if u == 0:
                nc.scalar.copy(result[:], bank[:])
            else:
                nc.vector.tensor_copy(result[:], bank[:])
            nc.sync.dma_start(out[:, cols], result[:])
